import numpy as np
import ml_dtypes


def mxq(x, axis, fmt="e4m3"):
    dtype, down = {"e4m3": (ml_dtypes.float8_e4m3fn, 7), "e5m2": (ml_dtypes.float8_e5m2, 14)}[fmt]
    v = np.moveaxis(np.asarray(x, np.float32).astype(ml_dtypes.bfloat16).astype(np.float64), axis, -1)
    blocks = v.reshape(v.shape[:-1] + (-1, 32))
    amax = np.abs(blocks).max(-1, keepdims=True)
    byte = np.maximum(np.where(amax > 0, np.frexp(amax)[1] - 1 + 127, 0) - down, 1)
    scale = np.exp2(byte - 127.0)
    codes = (blocks / scale).astype(np.float32).astype(dtype).astype(np.float64)
    return np.moveaxis((codes * scale).reshape(v.shape), -1, axis)


WIDE = False


def mx_kscale(k):
    if not WIDE:
        return np.ones(k)
    levels = np.array([30, -30])
    if k % 512:
        return np.exp2(np.random.permutation(np.resize(levels, k // 32))).repeat(32)
    a = np.empty((k // 512, 16))
    for p in range(k // 512):
        a[p, :8] = np.random.permutation(np.resize(levels, 8))
        for g in range(8):
            far = levels[np.abs(levels - a[p, g]) >= 10]
            a[p, g + 8] = far[np.random.randint(len(far))]
    return np.exp2(a.ravel()).repeat(32)


def f64(x):
    return np.asarray(x).astype(np.float64)


E2M1 = np.array([0.0, 0.5, 1.0, 1.5, 2.0, 3.0, 4.0, 6.0, -0.0, -0.5, -1.0, -1.5, -2.0, -3.0, -4.0, -6.0])


def pack_weight(w, fmt):
    k, n = w.shape
    w = f64(np.asarray(w, np.float32).astype(ml_dtypes.bfloat16)).reshape(k // 32, 32, n)
    amax = np.abs(w).max(1)
    if fmt == "e4m3":
        byte = np.frexp(amax)[1] - 1 + 127 - 7
    else:
        mant, ex = np.frexp(amax / 6.0)
        byte = np.where(mant > 0.5, ex, ex - 1) + 127
    byte = np.clip(np.where(amax > 0, byte, 1), 1, 254)
    scaled = (w * np.exp2(127.0 - byte)[:, None, :]).reshape(k, n).astype(np.float32)
    by_word = np.ascontiguousarray(scaled.reshape(k // 512, 128, 4, n).transpose(0, 1, 3, 2))
    if fmt == "e4m3":
        words = by_word.astype(ml_dtypes.float8_e4m3fn).view(np.uint8)
    else:
        c = by_word.astype(ml_dtypes.float4_e2m1fn).view(np.uint8) & 0xF
        words = (c[..., 0::2] | (c[..., 1::2] << 4)).reshape(k // 512, 128, 2 * n)
    return np.ascontiguousarray(words), np.ascontiguousarray(byte.astype(np.uint8).reshape(k // 512, 16, n))


def unpack_weight(words, scales, fmt):
    g, _, n = scales.shape
    words = np.ascontiguousarray(words).reshape(g, 128, n, -1)
    if fmt == "e4m3":
        vals = words.view(ml_dtypes.float8_e4m3fn).astype(np.float64)
    else:
        nib = np.empty((g, 128, n, 4), np.uint8)
        nib[..., 0::2] = words & 0xF
        nib[..., 1::2] = words >> 4
        vals = E2M1[nib]
    vals = vals * np.repeat(np.exp2(scales.astype(np.float64) - 127.0), 8, axis=1)[..., None]
    return vals.transpose(0, 1, 3, 2).reshape(g * 512, n)


def planes(y):
    n, m = y.shape
    v = y.astype(np.float32).astype(ml_dtypes.bfloat16).astype(np.float64).reshape(n // 32, 32, m)
    top = np.abs(v).max(1)
    byte = np.clip(np.where(top > 0, np.frexp(top)[1] - 1 + 127 - 7, 1), 1, 254)
    codes = (v * np.exp2(127.0 - byte)[:, None, :]).reshape(n, m).astype(np.float32).astype(ml_dtypes.float8_e4m3fn).view(np.uint8)
    words = codes.reshape(n // 512, 128, 4, m).transpose(0, 1, 3, 2)
    return np.ascontiguousarray(words), np.ascontiguousarray(byte.astype(np.uint8).reshape(n // 512, 16, m))


K, L, R, M, T = 1024, 1024, 512, 512, 1024


def setup_inputs():
    n = np.random.standard_normal
    s1 = mx_kscale(K)[:, None]
    s2 = mx_kscale(L)[:, None]
    u = mx_kscale(R)[:, None]
    p_w = pack_weight(n((R, M)) / np.sqrt(R) / u, "e2m1")
    return {
        "x": (n((K, T)) * s1).astype(np.float32),
        "wx": (n((K, R)) / np.sqrt(K) / s1 * u.T).astype(np.float32),
        "c": (n((L, T)) * s2).astype(np.float32),
        "wc": (n((L, R)) / np.sqrt(L) / s2).astype(np.float32),
        "w_words": p_w[0],
        "w_scales": p_w[1],
    }


def reference(x, wx, c, wc, w_words, w_scales):
    x_ = mxq(f64(x), 0, "e4m3")
    wx_ = mxq(f64(wx), 0, "e4m3")
    c_ = mxq(f64(c), 0, "e5m2")
    wc_ = mxq(f64(wc), 0, "e4m3")
    w_ = unpack_weight(w_words, w_scales, "e2m1")
    h_ = mxq((wx_.T @ x_) * (wc_.T @ c_), 0, "e4m3")
    y = w_.T @ h_
    out_0 = y
    return (out_0,) + planes(out_0)

@@ -1,0 +1,207 @@
+from contextlib import ExitStack
+
+import concourse.mybir as mybir
+
+K, L, R, M, T = 1024, 1024, 512, 512, 1024
+FLOPS = 2 * T * (K * R + L * R + R * M)
+
+F32 = mybir.dt.float32
+BF16 = mybir.dt.bfloat16
+I32 = mybir.dt.int32
+U32 = mybir.dt.uint32
+U8 = mybir.dt.uint8
+E4M3 = mybir.dt.float8_e4m3fn_x4
+E5M2 = mybir.dt.float8_e5m2_x4
+E2M1 = mybir.dt.float4_e2m1fn_x4
+
+P = 128
+PACK = 4
+K_PASS = P * PACK
+PASSES = 2
+HALF = 512
+CH = 128
+RUN = 4
+
+LOADS = [("wc", 0, 0, 512), ("wc", 1, 0, 512), ("c", 0, 0, 512), ("c", 1, 0, 512), ("wx", 0, 0, 512), ("wx", 1, 0, 512), ("x", 0, 0, 256), ("x", 1, 0, 256), ("x", 0, 256, 256), ("x", 1, 256, 256), ("c", 0, 512, 512), ("c", 1, 512, 512), ("x", 0, 512, 256), ("x", 1, 512, 256), ("x", 0, 768, 128), ("x", 1, 768, 128), ("x", 0, 896, 128), ("x", 1, 896, 128)]
+SHARE = {"wx0_0":1,"wx1_0":1,"x0_0":0,"x1_0":0.5,"x0_256":1,"x1_256":0,"c0_512":1,"c1_512":0.5,"x0_512":0,"x1_512":1,"x0_768":0.625,"x1_768":1,"x0_896":0.625,"x1_896":0,"wc0_0":0.5,"wc1_0":0.5}
+ENG = {"y4":"Sv","y5":"Sv","y7":"VS","pcc512_2":"V"}
+STORES = {0: 256, 256: 256, 512: 256, 768: 128, 896: 128}
+PX_BANK = ["a0","a1","c0","c1","a0","a1","c0","c1"]
+Y_BANK = ["b0","b1","b0","b1","b0","b1","c2","c3"]
+ORDER = "cVwc0_0 cSwc0_0 qwc0_0 deal cSwc1_0 cVwc1_0 cSc0_0 qwc1_0 cVc0_0 qc0_0 cSc1_0 cVc1_0 mc0_0_0 mc0_0_1 mc0_0_2 qc1_0 mc0_0_3 mc1_0_0 cVwx0_0 mc1_0_1 mc1_0_2 pcc0_0 mc1_0_3 pcc0_1 pcc0_2 qwx0_0 pcc0_3 cVwx1_0 cSx0_0 qwx1_0 cVx1_0 cSx1_0 qx0_0 qx1_0 cVx0_256 px0 px1 qx0_256 cSx1_256 mul0 hq0 mul1 y0 qx1_256 hq1 yb0 cVc0_512 px2 yc0 y1 px3 mul2 yc1 qc0_512 yb1 cVc1_512 cSc1_512 mc0_512_2 mc0_512_3 mul3 mc0_512_0 hq2 yq0 cSx0_512 mc0_512_1 yq1 qc1_512 y2 cVx1_512 yb2 mc1_512_0 mc1_512_1 hq3 cVx0_768 cSx0_768 mc1_512_2 qx0_512 pcc512_0 mc1_512_3 so0 qx1_512 pcc512_2 pcc512_1 px4 cVx1_768 pcc512_3 sq0 cVx0_896 y3 qx0_768 cSx0_896 qx1_768 px5 cSx1_896 mul4 px6 yc2 qx0_896 qx1_896 mul5 yc3 px7 hq4 yb3 hq5 so256 y4 mul6 y5 yq2 yc4 yq3 hq6 mul7 sq256 yc5 y6 yb4 hq7 so512 yc6 yb5 y7 yq4 yb6 yq5 yb7 so768 yq6 sq512 yc7 yq7 sq768 so896 sq896 ss"
+
+
+def tile_mix_bilin_fm_pl_none_kernel(tc, x, wx, c, wc, w_words, w_scales, out_0, out_1, out_2):
+    nc = tc.nc
+    src_of = {"x": x, "wx": wx, "c": c, "wc": wc}
+    with ExitStack() as ctx:
+        sb = ctx.enter_context(tc.tile_pool(name="sb", bufs=1))
+        ps = ctx.enter_context(tc.psum_pool(name="ps", bufs=1))
+        ctx.enter_context(tc.manual_schedule())
+
+        w_raw = sb.tile([P, 2 * M], U8, name="w_raw", align_bytes=64)
+        ws_raw = sb.tile([P, M], U8, name="ws_raw", align_bytes=64)
+        w_codes = sb.tile([P, 2 * M], U8, name="w_codes", align_bytes=64)
+        w_plane = sb.tile([P, M], U8, name="w_plane", align_bytes=64)
+        nc.vector.memset(ws_raw[:].bitcast(I32), 0)
+
+        raw, bf, codes, plane, width_of, piece_of = {}, {}, {}, {}, {}, {}
+        for name, g, t0, width in LOADS:
+            key = "%s%d_%d" % (name, g, t0)
+            width_of[key] = width
+            raw[key] = sb.tile([P, PACK, width], F32, name="raw_" + key)
+            bf[key] = sb.tile([P, PACK * width], BF16, name="bf_" + key, align_bytes=64)
+            codes[key] = sb.tile([P, width], U32, name="codes_" + key, align_bytes=64)
+            plane[key] = sb.tile([P, width], U8, name="plane_" + key, align_bytes=64)
+            if name == "x":
+                for t in range(t0, t0 + width, CH):
+                    piece_of[t // CH] = t0
+            rows = src_of[name][g * K_PASS : (g + 1) * K_PASS, t0 : t0 + width]
+            nc.sync.dma_start(out=raw[key][:], in_=rows.rearrange("(p j) w -> p j w", j=PACK))
+            if len(raw) == 1:
+                nc.scalar.dma_start(out=w_raw[:].bitcast(I32), in_=w_words[0].bitcast(I32))
+                for q in range(4):
+                    nc.scalar.dma_start(out=ws_raw[32 * q : 32 * q + 4, :].bitcast(I32), in_=w_scales[0, 4 * q : 4 * q + 4, :].bitcast(I32))
+
+        pc_sb = sb.tile([P, T // RUN, PACK, RUN], F32, name="pc_sb")
+        y_sb = sb.tile([P, PACK, T], F32, name="y_sb")
+        y_codes = sb.tile([P, T], U32, name="y_codes", align_bytes=64)
+        y_plane = sb.tile([P, T], U8, name="y_plane", align_bytes=64)
+        out_rows = out_0.rearrange("(p j) t -> p j t", j=PACK)
+        out_words = out_1[0].rearrange("p t i -> p (t i)").bitcast(I32)
+        pc_ps, px_ps, y_ps, h_bf, h_codes, h_plane, y_bf = {}, {}, {}, {}, {}, {}, {}
+
+        def copy_on(eng, out, in_):
+            if eng == "V":
+                nc.vector.tensor_copy(out=out, in_=in_)
+            else:
+                nc.scalar.copy(out=out, in_=in_)
+
+        def cast(eng, key):
+            share = SHARE.get(key, 0.625)
+            if key[0] == "w":
+                dst = bf[key][:].rearrange("p (i m j) -> p m j i", i=PACK, j=PACK)
+                src = raw[key][:].rearrange("p j (m i) -> p m j i", i=PACK)
+                cut = 2 if 0 < share < 1 else int(4 * share)
+                for i0 in range(0, cut, 2) if eng == "V" else range(cut, 4, 2):
+                    copy_on(eng, dst[:, :, :, i0 : i0 + 2], src[:, :, :, i0 : i0 + 2])
+                return
+            dst = bf[key][:].rearrange("p (c i j) -> p c j i", i=RUN, j=PACK)
+            src = raw[key][:].rearrange("p j (c i) -> p c j i", i=RUN)
+            n = width_of[key] // RUN
+            cut = int(n * share) // 2 * 2
+            part = slice(0, cut) if eng == "V" else slice(cut, n)
+            copy_on(eng, dst[:, part], src[:, part])
+
+        for step in ORDER.split():
+            if step == "deal":
+                nc.vector.tensor_copy(
+                    out=w_codes[:].rearrange("p (i m b) -> p i m b", i=PACK, b=2),
+                    in_=w_raw[:].rearrange("p (m i b) -> p i m b", i=PACK, b=2),
+                )
+                nc.vector.tensor_copy(
+                    out=w_plane[:].rearrange("p (i m) -> p i m", i=PACK),
+                    in_=ws_raw[:].rearrange("p (m i) -> p i m", i=PACK),
+                )
+            elif step.startswith("cV") or step.startswith("cS"):
+                cast(step[1], step[2:])
+            elif step.startswith("q"):
+                key = step[1:]
+                fmt = E5M2 if key[0] == "c" else E4M3
+                nc.vector.quantize_mx(out=codes[key][:].bitcast(fmt), scales=plane[key][:], in_=bf[key][:])
+            elif step.startswith("mc"):
+                g, t0, j = [int(v) for v in step[2:].split("_")]
+                if g == 0:
+                    pc_ps[t0, j] = ps.tile([P, HALF], F32, name="pc_%d_%d" % (t0, j), tag="c%d" % j)
+                cols = slice(j * P, (j + 1) * P)
+                wk, ck = "wc%d_0" % g, "c%d_%d" % (g, t0)
+                nc.tensor.matmul_mx(
+                    out=pc_ps[t0, j][:],
+                    lhsT=codes[wk][:, cols].bitcast(E4M3),
+                    lhsT_scale=plane[wk][:, cols],
+                    rhs=codes[ck][:].bitcast(E5M2),
+                    rhs_scale=plane[ck][:],
+                    start=(g == 0),
+                    stop=(g == PASSES - 1),
+                )
+            elif step.startswith("pcc"):
+                t0, j = [int(v) for v in step[3:].split("_")]
+                copy_on(
+                    ENG.get(step, "S"),
+                    pc_sb[:, t0 // RUN : (t0 + HALF) // RUN, j, :],
+                    pc_ps[t0, j][:].rearrange("p (c i) -> p c i", i=RUN),
+                )
+            elif step.startswith("px"):
+                e = int(step[2:])
+                p0 = piece_of[e]
+                mov = slice(e * CH - p0, (e + 1) * CH - p0)
+                px_ps[e] = ps.tile([P, PACK, CH], F32, name="px_%d" % e, tag=PX_BANK[e])
+                for j in range(PACK):
+                    cols = slice(j * P, (j + 1) * P)
+                    for g in range(PASSES):
+                        wk, xk = "wx%d_0" % g, "x%d_%d" % (g, p0)
+                        nc.tensor.matmul_mx(
+                            out=px_ps[e][:, j, :],
+                            lhsT=codes[wk][:, cols].bitcast(E4M3),
+                            lhsT_scale=plane[wk][:, cols],
+                            rhs=codes[xk][:, mov].bitcast(E4M3),
+                            rhs_scale=plane[xk][:, mov],
+                            start=(g == 0),
+                            stop=(g == PASSES - 1),
+                        )
+            elif step.startswith("mul"):
+                e = int(step[3:])
+                h_bf[e] = sb.tile([P, PACK * CH], BF16, name="h_bf_%d" % e, align_bytes=64)
+                nc.vector.tensor_tensor(
+                    out=h_bf[e][:].rearrange("p (c i j) -> p c j i", i=RUN, j=PACK),
+                    in0=px_ps[e][:].rearrange("p j (c i) -> p c j i", i=RUN),
+                    in1=pc_sb[:, e * CH // RUN : (e + 1) * CH // RUN],
+                    op=mybir.AluOpType.mult,
+                )
+            elif step.startswith("hq"):
+                e = int(step[2:])
+                h_codes[e] = sb.tile([P, CH], U32, name="h_codes_%d" % e, align_bytes=64)
+                h_plane[e] = sb.tile([P, CH], U8, name="h_plane_%d" % e, align_bytes=64)
+                nc.vector.quantize_mx(out=h_codes[e][:].bitcast(E4M3), scales=h_plane[e][:], in_=h_bf[e][:])
+            elif step.startswith("yb"):
+                e = int(step[2:])
+                mode = ENG.get("y%d" % e, "SS")
+                y_bf[e] = sb.tile([P, PACK * CH], BF16, name="y_bf_%d" % e, align_bytes=64)
+                if mode == "Sv":
+                    nc.vector.tensor_copy(
+                        out=y_bf[e][:].rearrange("p (c i j) -> p c j i", i=RUN, j=PACK),
+                        in_=y_sb[:, :, e * CH : (e + 1) * CH].rearrange("p j (c i) -> p c j i", i=RUN),
+                    )
+                else:
+                    copy_on(mode[0], y_bf[e][:].rearrange("p (t j) -> p t j", j=PACK), y_ps[e][:].rearrange("p j t -> p t j"))
+            elif step.startswith("yc"):
+                e = int(step[2:])
+                mode = ENG.get("y%d" % e, "SS")
+                copy_on("S" if mode == "Sv" else mode[1], y_sb[:, :, e * CH : (e + 1) * CH], y_ps[e][:])
+            elif step.startswith("yq"):
+                e = int(step[2:])
+                cols = slice(e * CH, (e + 1) * CH)
+                nc.vector.quantize_mx(out=y_codes[:, cols].bitcast(E4M3), scales=y_plane[:, cols], in_=y_bf[e][:])
+            elif step.startswith("y"):
+                e = int(step[1:])
+                y_ps[e] = ps.tile([P, PACK, CH], F32, name="y_%d" % e, tag=Y_BANK[e])
+                for j in range(PACK):
+                    nc.tensor.matmul_mx(
+                        out=y_ps[e][:, j, :],
+                        lhsT=w_codes[:, 2 * j * P : 2 * (j + 1) * P].bitcast(E2M1),
+                        lhsT_scale=w_plane[:, j * P : (j + 1) * P],
+                        rhs=h_codes[e][:].bitcast(E4M3),
+                        rhs_scale=h_plane[e][:],
+                        start=True,
+                        stop=True,
+                    )
+            elif step.startswith("so"):
+                t0 = int(step[2:])
+                nc.sync.dma_start(out=out_rows[:, :, t0 : t0 + STORES[t0]], in_=y_sb[:, :, t0 : t0 + STORES[t0]])
+            elif step.startswith("sq"):
+                t0 = int(step[2:])
+                nc.sync.dma_start(out=out_words[:, t0 : t0 + STORES[t0]], in_=y_codes[:, t0 : t0 + STORES[t0]].bitcast(I32))
+            else:
+                for q in range(4):
+                    eng = nc.scalar if q % 2 else nc.sync
+                    eng.dma_start(out=out_2[0, 4 * q : 4 * q + 4, :].bitcast(I32), in_=y_plane[32 * q : 32 * q + 4, :].bitcast(I32))

@@ -17,191 +17,308 @@ E2M1 = mybir.dt.float4_e2m1fn_x4
 P = 128
 PACK = 4
 K_PASS = P * PACK
-PASSES = 2
+PASSES = K // K_PASS
 HALF = 512
-CH = 128
+CHUNK = 128
 RUN = 4
+QUADS = 4
 
-LOADS = [("wc", 0, 0, 512), ("wc", 1, 0, 512), ("c", 0, 0, 512), ("c", 1, 0, 512), ("wx", 0, 0, 512), ("wx", 1, 0, 512), ("x", 0, 0, 256), ("x", 1, 0, 256), ("x", 0, 256, 256), ("x", 1, 256, 256), ("c", 0, 512, 512), ("c", 1, 512, 512), ("x", 0, 512, 256), ("x", 1, 512, 256), ("x", 0, 768, 128), ("x", 1, 768, 128), ("x", 0, 896, 128), ("x", 1, 896, 128)]
-SHARE = {"wx0_0":1,"wx1_0":1,"x0_0":0,"x1_0":0.5,"x0_256":1,"x1_256":0,"c0_512":1,"c1_512":0.5,"x0_512":0,"x1_512":1,"x0_768":0.625,"x1_768":1,"x0_896":0.625,"x1_896":0,"wc0_0":0.5,"wc1_0":0.5}
-ENG = {"y4":"Sv","y5":"Sv","y7":"VS","pcc512_2":"V"}
-STORES = {0: 256, 256: 256, 512: 256, 768: 128, 896: 128}
-PX_BANK = ["a0","a1","c0","c1","a0","a1","c0","c1"]
-Y_BANK = ["b0","b1","b0","b1","b0","b1","c2","c3"]
-ORDER = "cVwc0_0 cSwc0_0 qwc0_0 deal cSwc1_0 cVwc1_0 cSc0_0 qwc1_0 cVc0_0 qc0_0 cSc1_0 cVc1_0 mc0_0_0 mc0_0_1 mc0_0_2 qc1_0 mc0_0_3 mc1_0_0 cVwx0_0 mc1_0_1 mc1_0_2 pcc0_0 mc1_0_3 pcc0_1 pcc0_2 qwx0_0 pcc0_3 cVwx1_0 cSx0_0 qwx1_0 cVx1_0 cSx1_0 qx0_0 qx1_0 cVx0_256 px0 px1 qx0_256 cSx1_256 mul0 hq0 mul1 y0 qx1_256 hq1 yb0 cVc0_512 px2 yc0 y1 px3 mul2 yc1 qc0_512 yb1 cVc1_512 cSc1_512 mc0_512_2 mc0_512_3 mul3 mc0_512_0 hq2 yq0 cSx0_512 mc0_512_1 yq1 qc1_512 y2 cVx1_512 yb2 mc1_512_0 mc1_512_1 hq3 cVx0_768 cSx0_768 mc1_512_2 qx0_512 pcc512_0 mc1_512_3 so0 qx1_512 pcc512_2 pcc512_1 px4 cVx1_768 pcc512_3 sq0 cVx0_896 y3 qx0_768 cSx0_896 qx1_768 px5 cSx1_896 mul4 px6 yc2 qx0_896 qx1_896 mul5 yc3 px7 hq4 yb3 hq5 so256 y4 mul6 y5 yq2 yc4 yq3 hq6 mul7 sq256 yc5 y6 yb4 hq7 so512 yc6 yb5 y7 yq4 yb6 yq5 yb7 so768 yq6 sq512 yc7 yq7 sq768 so896 sq896 ss"
+X_LOADS = [(0, 0, 512), (1, 0, 256), (1, 256, 256), (0, 512, 512), (1, 512, 256), (1, 768, 128), (1, 896, 128)]
+X_PIECE = 256
+
+SHARE, SHARE_LARGE, SHARE_EVEN = 5, 6, 4
 
 
 def tile_mix_bilin_fm_pl_none_kernel(tc, x, wx, c, wc, w_words, w_scales, out_0, out_1, out_2):
     nc = tc.nc
-    src_of = {"x": x, "wx": wx, "c": c, "wc": wc}
     with ExitStack() as ctx:
         sb = ctx.enter_context(tc.tile_pool(name="sb", bufs=1))
         ps = ctx.enter_context(tc.psum_pool(name="ps", bufs=1))
         ctx.enter_context(tc.manual_schedule())
 
-        w_raw = sb.tile([P, 2 * M], U8, name="w_raw", align_bytes=64)
-        ws_raw = sb.tile([P, M], U8, name="ws_raw", align_bytes=64)
-        w_codes = sb.tile([P, 2 * M], U8, name="w_codes", align_bytes=64)
-        w_plane = sb.tile([P, M], U8, name="w_plane", align_bytes=64)
-        nc.vector.memset(ws_raw[:].bitcast(I32), 0)
+        raw, rounded, words, planes = {}, {}, {}, {}
+        x_piece_of = {}
 
-        raw, bf, codes, plane, width_of, piece_of = {}, {}, {}, {}, {}, {}
-        for name, g, t0, width in LOADS:
-            key = "%s%d_%d" % (name, g, t0)
-            width_of[key] = width
-            raw[key] = sb.tile([P, PACK, width], F32, name="raw_" + key)
-            bf[key] = sb.tile([P, PACK * width], BF16, name="bf_" + key, align_bytes=64)
-            codes[key] = sb.tile([P, width], U32, name="codes_" + key, align_bytes=64)
-            plane[key] = sb.tile([P, width], U8, name="plane_" + key, align_bytes=64)
-            if name == "x":
-                for t in range(t0, t0 + width, CH):
-                    piece_of[t // CH] = t0
-            rows = src_of[name][g * K_PASS : (g + 1) * K_PASS, t0 : t0 + width]
-            nc.sync.dma_start(out=raw[key][:], in_=rows.rearrange("(p j) w -> p j w", j=PACK))
-            if len(raw) == 1:
-                nc.scalar.dma_start(out=w_raw[:].bitcast(I32), in_=w_words[0].bitcast(I32))
-                for q in range(4):
-                    nc.scalar.dma_start(out=ws_raw[32 * q : 32 * q + 4, :].bitcast(I32), in_=w_scales[0, 4 * q : 4 * q + 4, :].bitcast(I32))
+        def declare(piece, values):
+            label = "%s_%d_%d" % piece
+            width = values.shape[2]
+            raw[piece] = values
+            rounded[piece] = sb.tile([P, PACK * width], BF16, name="rounded_" + label, align_bytes=64)
+            words[piece] = sb.tile([P, width], U32, name="words_" + label, align_bytes=64)
+            planes[piece] = sb.tile([P, width], U8, name="plane_" + label, align_bytes=64)
 
+        def load(name, src, g, t0, width, piece_width):
+            landed = sb.tile([P, PACK, width], F32, name="raw_%s_%d_%d" % (name, g, t0))
+            rows = src[g * K_PASS : (g + 1) * K_PASS, t0 : t0 + width]
+            nc.sync.dma_start(out=landed[:], in_=rows.rearrange("(p j) w -> p j w", j=PACK))
+            for p0 in range(0, width, piece_width):
+                declare((name, g, t0 + p0), landed[:, :, p0 : p0 + piece_width])
+
+        w_plane_raw = sb.tile([P, M], U8, name="w_plane_raw", align_bytes=64)
+        nc.vector.memset(w_plane_raw[:].bitcast(I32), 0)
+
+        wc_raw = sb.tile([P, PASSES, PACK, R], F32, name="wc_raw")
+        nc.sync.dma_start(
+            out=wc_raw[:].rearrange("p g j r -> p g (j r)"),
+            in_=wc.rearrange("(g p j) r -> p g (j r)", g=PASSES, j=PACK),
+        )
+        for g in range(PASSES):
+            declare(("wc", g, 0), wc_raw[:, g])
+
+        w_words_raw = sb.tile([P, 2 * M], U8, name="w_words_raw", align_bytes=64)
+        nc.scalar.dma_start(out=w_words_raw[:].bitcast(I32), in_=w_words[0].bitcast(I32))
+        for quad in range(QUADS):
+            nc.scalar.dma_start(
+                out=w_plane_raw[32 * quad : 32 * quad + 4, :].bitcast(I32),
+                in_=w_scales[0, 4 * quad : 4 * quad + 4, :].bitcast(I32),
+            )
+
+        for g in range(PASSES):
+            load("c", c, g, 0, T, HALF)
+        for g in range(PASSES):
+            load("wx", wx, g, 0, R, R)
+        for g, t0, width in X_LOADS:
+            piece_width = min(width, X_PIECE)
+            load("x", x, g, t0, width, piece_width)
+            for t in range(t0, t0 + width, CHUNK):
+                x_piece_of[g, t // CHUNK] = t0 + (t - t0) // piece_width * piece_width
+
+        def round_weight(piece):
+            dst = rounded[piece][:].rearrange("p (i m j) -> p m j i", i=PACK, j=PACK)
+            src = raw[piece].rearrange("p j (m i) -> p m j i", i=PACK)
+            nc.vector.tensor_copy(out=dst[:, :, :, 0:2], in_=src[:, :, :, 0:2])
+            nc.scalar.copy(out=dst[:, :, :, 2:4], in_=src[:, :, :, 2:4])
+
+        def run_views(piece):
+            dst = rounded[piece][:].rearrange("p (c i j) -> p c j i", i=RUN, j=PACK)
+            return dst, raw[piece].rearrange("p j (c i) -> p c j i", i=RUN)
+
+        def round_on_vector(piece, eighths):
+            dst, src = run_views(piece)
+            cut = dst.shape[1] * eighths // 8
+            nc.vector.tensor_copy(out=dst[:, :cut], in_=src[:, :cut])
+
+        def round_on_scalar(piece, eighths):
+            dst, src = run_views(piece)
+            cut = dst.shape[1] * eighths // 8
+            nc.scalar.copy(out=dst[:, cut:], in_=src[:, cut:])
+
+        def round_shared(piece):
+            round_on_vector(piece, SHARE)
+            round_on_scalar(piece, SHARE)
+
+        def quantise(piece):
+            fmt = E5M2 if piece[0] == "c" else E4M3
+            nc.vector.quantize_mx(out=words[piece][:].bitcast(fmt), scales=planes[piece][:], in_=rounded[piece][:])
+
+        pc_bank, px_bank, y_bank = {}, {}, {}
         pc_sb = sb.tile([P, T // RUN, PACK, RUN], F32, name="pc_sb")
         y_sb = sb.tile([P, PACK, T], F32, name="y_sb")
-        y_codes = sb.tile([P, T], U32, name="y_codes", align_bytes=64)
+        y_words = sb.tile([P, T], U32, name="y_words", align_bytes=64)
         y_plane = sb.tile([P, T], U8, name="y_plane", align_bytes=64)
-        out_rows = out_0.rearrange("(p j) t -> p j t", j=PACK)
-        out_words = out_1[0].rearrange("p t i -> p (t i)").bitcast(I32)
-        pc_ps, px_ps, y_ps, h_bf, h_codes, h_plane, y_bf = {}, {}, {}, {}, {}, {}, {}
+        h_rounded, h_words, h_plane, y_rounded = {}, {}, {}, {}
+        w_words_dealt = sb.tile([P, 2 * M], U8, name="w_words_dealt", align_bytes=64)
+        w_plane_dealt = sb.tile([P, M], U8, name="w_plane_dealt", align_bytes=64)
 
-        def copy_on(eng, out, in_):
-            if eng == "V":
-                nc.vector.tensor_copy(out=out, in_=in_)
-            else:
-                nc.scalar.copy(out=out, in_=in_)
-
-        def cast(eng, key):
-            share = SHARE.get(key, 0.625)
-            if key[0] == "w":
-                dst = bf[key][:].rearrange("p (i m j) -> p m j i", i=PACK, j=PACK)
-                src = raw[key][:].rearrange("p j (m i) -> p m j i", i=PACK)
-                cut = 2 if 0 < share < 1 else int(4 * share)
-                for i0 in range(0, cut, 2) if eng == "V" else range(cut, 4, 2):
-                    copy_on(eng, dst[:, :, :, i0 : i0 + 2], src[:, :, :, i0 : i0 + 2])
-                return
-            dst = bf[key][:].rearrange("p (c i j) -> p c j i", i=RUN, j=PACK)
-            src = raw[key][:].rearrange("p j (c i) -> p c j i", i=RUN)
-            n = width_of[key] // RUN
-            cut = int(n * share) // 2 * 2
-            part = slice(0, cut) if eng == "V" else slice(cut, n)
-            copy_on(eng, dst[:, part], src[:, part])
-
-        for step in ORDER.split():
-            if step == "deal":
-                nc.vector.tensor_copy(
-                    out=w_codes[:].rearrange("p (i m b) -> p i m b", i=PACK, b=2),
-                    in_=w_raw[:].rearrange("p (m i b) -> p i m b", i=PACK, b=2),
-                )
-                nc.vector.tensor_copy(
-                    out=w_plane[:].rearrange("p (i m) -> p i m", i=PACK),
-                    in_=ws_raw[:].rearrange("p (m i) -> p i m", i=PACK),
-                )
-            elif step.startswith("cV") or step.startswith("cS"):
-                cast(step[1], step[2:])
-            elif step.startswith("q"):
-                key = step[1:]
-                fmt = E5M2 if key[0] == "c" else E4M3
-                nc.vector.quantize_mx(out=codes[key][:].bitcast(fmt), scales=plane[key][:], in_=bf[key][:])
-            elif step.startswith("mc"):
-                g, t0, j = [int(v) for v in step[2:].split("_")]
-                if g == 0:
-                    pc_ps[t0, j] = ps.tile([P, HALF], F32, name="pc_%d_%d" % (t0, j), tag="c%d" % j)
-                cols = slice(j * P, (j + 1) * P)
-                wk, ck = "wc%d_0" % g, "c%d_%d" % (g, t0)
-                nc.tensor.matmul_mx(
-                    out=pc_ps[t0, j][:],
-                    lhsT=codes[wk][:, cols].bitcast(E4M3),
-                    lhsT_scale=plane[wk][:, cols],
-                    rhs=codes[ck][:].bitcast(E5M2),
-                    rhs_scale=plane[ck][:],
-                    start=(g == 0),
-                    stop=(g == PASSES - 1),
-                )
-            elif step.startswith("pcc"):
-                t0, j = [int(v) for v in step[3:].split("_")]
-                copy_on(
-                    ENG.get(step, "S"),
-                    pc_sb[:, t0 // RUN : (t0 + HALF) // RUN, j, :],
-                    pc_ps[t0, j][:].rearrange("p (c i) -> p c i", i=RUN),
-                )
-            elif step.startswith("px"):
-                e = int(step[2:])
-                p0 = piece_of[e]
-                mov = slice(e * CH - p0, (e + 1) * CH - p0)
-                px_ps[e] = ps.tile([P, PACK, CH], F32, name="px_%d" % e, tag=PX_BANK[e])
-                for j in range(PACK):
-                    cols = slice(j * P, (j + 1) * P)
-                    for g in range(PASSES):
-                        wk, xk = "wx%d_0" % g, "x%d_%d" % (g, p0)
-                        nc.tensor.matmul_mx(
-                            out=px_ps[e][:, j, :],
-                            lhsT=codes[wk][:, cols].bitcast(E4M3),
-                            lhsT_scale=plane[wk][:, cols],
-                            rhs=codes[xk][:, mov].bitcast(E4M3),
-                            rhs_scale=plane[xk][:, mov],
-                            start=(g == 0),
-                            stop=(g == PASSES - 1),
-                        )
-            elif step.startswith("mul"):
-                e = int(step[3:])
-                h_bf[e] = sb.tile([P, PACK * CH], BF16, name="h_bf_%d" % e, align_bytes=64)
-                nc.vector.tensor_tensor(
-                    out=h_bf[e][:].rearrange("p (c i j) -> p c j i", i=RUN, j=PACK),
-                    in0=px_ps[e][:].rearrange("p j (c i) -> p c j i", i=RUN),
-                    in1=pc_sb[:, e * CH // RUN : (e + 1) * CH // RUN],
-                    op=mybir.AluOpType.mult,
-                )
-            elif step.startswith("hq"):
-                e = int(step[2:])
-                h_codes[e] = sb.tile([P, CH], U32, name="h_codes_%d" % e, align_bytes=64)
-                h_plane[e] = sb.tile([P, CH], U8, name="h_plane_%d" % e, align_bytes=64)
-                nc.vector.quantize_mx(out=h_codes[e][:].bitcast(E4M3), scales=h_plane[e][:], in_=h_bf[e][:])
-            elif step.startswith("yb"):
-                e = int(step[2:])
-                mode = ENG.get("y%d" % e, "SS")
-                y_bf[e] = sb.tile([P, PACK * CH], BF16, name="y_bf_%d" % e, align_bytes=64)
-                if mode == "Sv":
-                    nc.vector.tensor_copy(
-                        out=y_bf[e][:].rearrange("p (c i j) -> p c j i", i=RUN, j=PACK),
-                        in_=y_sb[:, :, e * CH : (e + 1) * CH].rearrange("p j (c i) -> p c j i", i=RUN),
-                    )
-                else:
-                    copy_on(mode[0], y_bf[e][:].rearrange("p (t j) -> p t j", j=PACK), y_ps[e][:].rearrange("p j t -> p t j"))
-            elif step.startswith("yc"):
-                e = int(step[2:])
-                mode = ENG.get("y%d" % e, "SS")
-                copy_on("S" if mode == "Sv" else mode[1], y_sb[:, :, e * CH : (e + 1) * CH], y_ps[e][:])
-            elif step.startswith("yq"):
-                e = int(step[2:])
-                cols = slice(e * CH, (e + 1) * CH)
-                nc.vector.quantize_mx(out=y_codes[:, cols].bitcast(E4M3), scales=y_plane[:, cols], in_=y_bf[e][:])
-            elif step.startswith("y"):
-                e = int(step[1:])
-                y_ps[e] = ps.tile([P, PACK, CH], F32, name="y_%d" % e, tag=Y_BANK[e])
-                for j in range(PACK):
+        def project_c(half):
+            for i in range(PACK):
+                pc_bank[half, i] = ps.tile([P, HALF], F32, name="pc_%d_%d" % (half, i), tag="bank%d" % (PACK * half + i))
+                dealt = slice(i * P, (i + 1) * P)
+                for g in range(PASSES):
                     nc.tensor.matmul_mx(
-                        out=y_ps[e][:, j, :],
-                        lhsT=w_codes[:, 2 * j * P : 2 * (j + 1) * P].bitcast(E2M1),
-                        lhsT_scale=w_plane[:, j * P : (j + 1) * P],
-                        rhs=h_codes[e][:].bitcast(E4M3),
-                        rhs_scale=h_plane[e][:],
-                        start=True,
-                        stop=True,
+                        out=pc_bank[half, i][:],
+                        lhsT=words["wc", g, 0][:, dealt].bitcast(E4M3),
+                        lhsT_scale=planes["wc", g, 0][:, dealt],
+                        rhs=words["c", g, half * HALF][:].bitcast(E5M2),
+                        rhs_scale=planes["c", g, half * HALF][:],
+                        start=(g == 0),
+                        stop=(g == PASSES - 1),
                     )
-            elif step.startswith("so"):
-                t0 = int(step[2:])
-                nc.sync.dma_start(out=out_rows[:, :, t0 : t0 + STORES[t0]], in_=y_sb[:, :, t0 : t0 + STORES[t0]])
-            elif step.startswith("sq"):
-                t0 = int(step[2:])
-                nc.sync.dma_start(out=out_words[:, t0 : t0 + STORES[t0]], in_=y_codes[:, t0 : t0 + STORES[t0]].bitcast(I32))
-            else:
-                for q in range(4):
-                    eng = nc.scalar if q % 2 else nc.sync
-                    eng.dma_start(out=out_2[0, 4 * q : 4 * q + 4, :].bitcast(I32), in_=y_plane[32 * q : 32 * q + 4, :].bitcast(I32))
+
+        def empty_pc(half, i):
+            runs = slice(half * HALF // RUN, (half + 1) * HALF // RUN)
+            nc.scalar.copy(out=pc_sb[:, runs, i, :], in_=pc_bank[half, i][:].rearrange("p (c u) -> p c u", u=RUN))
+
+        def project_x(e):
+            px_bank[e] = ps.tile([P, PACK, CHUNK], F32, name="px_%d" % e, tag="bank%d" % (e % PACK))
+            for i in range(PACK):
+                dealt = slice(i * P, (i + 1) * P)
+                for g in range(PASSES):
+                    p0 = x_piece_of[g, e]
+                    cols = slice(e * CHUNK - p0, (e + 1) * CHUNK - p0)
+                    nc.tensor.matmul_mx(
+                        out=px_bank[e][:, i, :],
+                        lhsT=words["wx", g, 0][:, dealt].bitcast(E4M3),
+                        lhsT_scale=planes["wx", g, 0][:, dealt],
+                        rhs=words["x", g, p0][:, cols].bitcast(E4M3),
+                        rhs_scale=planes["x", g, p0][:, cols],
+                        start=(g == 0),
+                        stop=(g == PASSES - 1),
+                    )
+
+        def multiply(e):
+            h_rounded[e] = sb.tile([P, PACK * CHUNK], BF16, name="h_rounded_%d" % e, align_bytes=64)
+            nc.vector.tensor_tensor(
+                out=h_rounded[e][:].rearrange("p (c u i) -> p c i u", u=RUN, i=PACK),
+                in0=px_bank[e][:].rearrange("p i (c u) -> p c i u", u=RUN),
+                in1=pc_sb[:, e * CHUNK // RUN : (e + 1) * CHUNK // RUN],
+                op=mybir.AluOpType.mult,
+            )
+
+        def project_h(e):
+            h_words[e] = sb.tile([P, CHUNK], U32, name="h_words_%d" % e, align_bytes=64)
+            h_plane[e] = sb.tile([P, CHUNK], U8, name="h_plane_%d" % e, align_bytes=64)
+            nc.vector.quantize_mx(out=h_words[e][:].bitcast(E4M3), scales=h_plane[e][:], in_=h_rounded[e][:])
+            y_bank[e] = ps.tile([P, PACK, CHUNK], F32, name="y_%d" % e, tag="bank%d" % (PACK + e % PACK))
+            for i in range(PACK):
+                nc.tensor.matmul_mx(
+                    out=y_bank[e][:, i, :],
+                    lhsT=w_words_dealt[:, 2 * i * P : 2 * (i + 1) * P].bitcast(E2M1),
+                    lhsT_scale=w_plane_dealt[:, i * P : (i + 1) * P],
+                    rhs=h_words[e][:].bitcast(E4M3),
+                    rhs_scale=h_plane[e][:],
+                    start=True,
+                    stop=True,
+                )
+
+        def deal_w():
+            nc.vector.tensor_copy(
+                out=w_words_dealt[:].rearrange("p (i m b) -> p i m b", i=PACK, b=2),
+                in_=w_words_raw[:].rearrange("p (m i b) -> p i m b", i=PACK, b=2),
+            )
+            nc.vector.tensor_copy(
+                out=w_plane_dealt[:].rearrange("p (i m) -> p i m", i=PACK),
+                in_=w_plane_raw[:].rearrange("p (m i) -> p i m", i=PACK),
+            )
+
+        def copy_y(e):
+            nc.scalar.copy(out=y_sb[:, :, e * CHUNK : (e + 1) * CHUNK], in_=y_bank[e][:])
+
+        def round_y_from_psum(e):
+            y_rounded[e] = sb.tile([P, PACK * CHUNK], BF16, name="y_rounded_%d" % e, align_bytes=64)
+            nc.scalar.copy(out=y_rounded[e][:].rearrange("p (t i) -> p t i", i=PACK), in_=y_bank[e][:].rearrange("p i t -> p t i"))
+
+        def round_y_from_sbuf(e):
+            y_rounded[e] = sb.tile([P, PACK * CHUNK], BF16, name="y_rounded_%d" % e, align_bytes=64)
+            nc.vector.tensor_copy(
+                out=y_rounded[e][:].rearrange("p (c u i) -> p c i u", u=RUN, i=PACK),
+                in_=y_sb[:, :, e * CHUNK : (e + 1) * CHUNK].rearrange("p i (c u) -> p c i u", u=RUN),
+            )
+
+        def quantise_y(e):
+            cols = slice(e * CHUNK, (e + 1) * CHUNK)
+            nc.vector.quantize_mx(out=y_words[:, cols].bitcast(E4M3), scales=y_plane[:, cols], in_=y_rounded[e][:])
+
+        def store_values(first, last):
+            cols = slice(first * CHUNK, (last + 1) * CHUNK)
+            nc.sync.dma_start(out=out_0.rearrange("(p i) t -> p i t", i=PACK)[:, :, cols], in_=y_sb[:, :, cols])
+
+        def store_words(queue, first, last):
+            cols = slice(first * CHUNK, (last + 1) * CHUNK)
+            queue.dma_start(out=out_1[0].rearrange("p t i -> p (t i)").bitcast(I32)[:, cols], in_=y_words[:, cols].bitcast(I32))
+
+        for g in range(PASSES):
+            round_weight(("wc", g, 0))
+        for g in range(PASSES):
+            quantise(("wc", g, 0))
+        for t0 in (0, HALF):
+            round_shared(("c", 0, t0))
+        for t0 in (0, HALF):
+            quantise(("c", 0, t0))
+        deal_w()
+        for t0 in (0, HALF):
+            round_shared(("c", 1, t0))
+        quantise(("c", 1, 0))
+        project_c(0)
+        round_weight(("wx", 0, 0))
+        quantise(("c", 1, HALF))
+        project_c(1)
+        quantise(("wx", 0, 0))
+        empty_pc(0, 0)
+        round_weight(("wx", 1, 0))
+        quantise(("wx", 1, 0))
+        empty_pc(0, 1)
+        empty_pc(0, 2)
+
+        round_shared(("x", 0, 0))
+        round_shared(("x", 0, 256))
+        quantise(("x", 0, 0))
+        empty_pc(0, 3)
+        round_shared(("x", 1, 0))
+        quantise(("x", 0, 256))
+        quantise(("x", 1, 0))
+        project_x(0)
+        project_x(1)
+        empty_pc(1, 0)
+        round_shared(("x", 1, 256))
+        quantise(("x", 1, 256))
+        project_x(2)
+        project_x(3)
+        for i in range(1, PACK):
+            empty_pc(1, i)
+        multiply(0)
+        for e in range(3):
+            multiply(e + 1)
+            project_h(e)
+
+        round_on_scalar(("x", 0, 512), 0)
+        round_on_scalar(("x", 0, 768), SHARE_EVEN)
+        round_on_scalar(("x", 1, 512), SHARE_LARGE)
+        round_on_vector(("x", 1, 512), SHARE_LARGE)
+        project_h(3)
+        quantise(("x", 0, 512))
+        quantise(("x", 1, 512))
+        project_x(4)
+        project_x(5)
+        round_on_vector(("x", 1, 768), 8)
+        round_on_vector(("x", 0, 768), SHARE_EVEN)
+        quantise(("x", 1, 768))
+        round_on_vector(("x", 1, 896), 8)
+        quantise(("x", 0, 768))
+        quantise(("x", 1, 896))
+        project_x(6)
+        project_x(7)
+        for e in range(4):
+            copy_y(e)
+        store_values(0, 1)
+        store_values(2, 3)
+        for e in range(4):
+            round_y_from_psum(e)
+
+        multiply(4)
+        multiply(5)
+        project_h(4)
+        quantise_y(0)
+        quantise_y(1)
+        project_h(5)
+        multiply(6)
+        quantise_y(2)
+        quantise_y(3)
+        store_words(nc.sync, 0, 3)
+        project_h(6)
+        multiply(7)
+        copy_y(4)
+        round_y_from_sbuf(4)
+        project_h(7)
+        copy_y(5)
+        store_values(4, 5)
+        round_y_from_sbuf(5)
+        quantise_y(4)
+        quantise_y(5)
+        copy_y(6)
+        store_values(6, 6)
+        round_y_from_psum(6)
+        quantise_y(6)
+        store_words(nc.sync, 4, 6)
+        round_y_from_psum(7)
+        copy_y(7)
+        quantise_y(7)
+
+        store_values(7, 7)
+        store_words(nc.scalar, 7, 7)
+        for quad in range(QUADS):
+            queue = nc.scalar if quad % 2 else nc.sync
+            queue.dma_start(
+                out=out_2[0, 4 * quad : 4 * quad + 4, :].bitcast(I32),
+                in_=y_plane[32 * quad : 32 * quad + 4, :].bitcast(I32),
+            )

@@ -21,6 +21,7 @@ PASSES = K // K_PASS
 HALF = 512
 CHUNK = 128
 RUN = 4
+PAIR = 2
 QUADS = 4
 
 X_LOADS = [(0, 0, 512), (1, 0, 256), (1, 256, 256), (0, 512, 512), (1, 512, 256), (1, 768, 128), (1, 896, 128)]
@@ -90,8 +91,8 @@ def tile_mix_bilin_fm_pl_none_kernel(tc, x, wx, c, wc, w_words, w_scales, out_0,
             nc.scalar.copy(out=dst[:, :, :, 2:4], in_=src[:, :, :, 2:4])
 
         def run_views(piece):
-            dst = rounded[piece][:].rearrange("p (c i j) -> p c j i", i=RUN, j=PACK)
-            return dst, raw[piece].rearrange("p j (c i) -> p c j i", i=RUN)
+            dst = rounded[piece][:].rearrange("p (c i j) -> p c j i", i=PAIR, j=PACK)
+            return dst, raw[piece].rearrange("p j (c i) -> p c j i", i=PAIR)
 
         def round_on_vector(piece, eighths):
             dst, src = run_views(piece)
@@ -201,8 +202,8 @@ def tile_mix_bilin_fm_pl_none_kernel(tc, x, wx, c, wc, w_words, w_scales, out_0,
         def round_y_from_sbuf(e):
             y_rounded[e] = sb.tile([P, PACK * CHUNK], BF16, name="y_rounded_%d" % e, align_bytes=64)
             nc.vector.tensor_copy(
-                out=y_rounded[e][:].rearrange("p (c u i) -> p c i u", u=RUN, i=PACK),
-                in_=y_sb[:, :, e * CHUNK : (e + 1) * CHUNK].rearrange("p i (c u) -> p c i u", u=RUN),
+                out=y_rounded[e][:].rearrange("p (c u i) -> p c i u", u=PAIR, i=PACK),
+                in_=y_sb[:, :, e * CHUNK : (e + 1) * CHUNK].rearrange("p i (c u) -> p c i u", u=PAIR),
             )
 
         def quantise_y(e):

@@ -116,7 +116,7 @@ def tile_mix_bilin_fm_pl_none_kernel(tc, x, wx, c, wc, w_words, w_scales, out_0,
         pc_sb = sb.tile([P, T // RUN, PACK, RUN], F32, name="pc_sb")
         y_sb = sb.tile([P, PACK, T], F32, name="y_sb")
         y_words = sb.tile([P, T], U32, name="y_words", align_bytes=64)
-        y_plane = sb.tile([P, T], U8, name="y_plane", align_bytes=64)
+        y_plane = sb.tile([P, T // PACK], U8, name="y_plane", align_bytes=64)
         h_rounded, h_words, h_plane, y_rounded = {}, {}, {}, {}
         w_words_dealt = sb.tile([P, 2 * M], U8, name="w_words_dealt", align_bytes=64)
         w_plane_dealt = sb.tile([P, M], U8, name="w_plane_dealt", align_bytes=64)
@@ -208,7 +208,9 @@ def tile_mix_bilin_fm_pl_none_kernel(tc, x, wx, c, wc, w_words, w_scales, out_0,
 
         def quantise_y(e):
             cols = slice(e * CHUNK, (e + 1) * CHUNK)
-            nc.vector.quantize_mx(out=y_words[:, cols].bitcast(E4M3), scales=y_plane[:, cols], in_=y_rounded[e][:])
+            k, first = divmod(e * CHUNK, T // PACK)
+            scales = y_plane[4 * k :, first : first + CHUNK]
+            nc.vector.quantize_mx(out=y_words[:, cols].bitcast(E4M3), scales=scales, in_=y_rounded[e][:])
 
         def store_values(first, last):
             cols = slice(first * CHUNK, (last + 1) * CHUNK)
@@ -316,10 +318,9 @@ def tile_mix_bilin_fm_pl_none_kernel(tc, x, wx, c, wc, w_words, w_scales, out_0,
         quantise_y(7)
 
         store_values(7, 7)
-        store_words(nc.scalar, 7, 7)
         for quad in range(QUADS):
-            queue = nc.scalar if quad % 2 else nc.sync
-            queue.dma_start(
-                out=out_2[0, 4 * quad : 4 * quad + 4, :].bitcast(I32),
-                in_=y_plane[32 * quad : 32 * quad + 4, :].bitcast(I32),
+            nc.scalar.dma_start(
+                out=out_2[0, 4 * quad : 4 * quad + 4, :].bitcast(I32).rearrange("s (k c) -> k s c", k=PACK),
+                in_=y_plane[32 * quad : 32 * quad + 16, :].bitcast(I32),
             )
+        store_words(nc.scalar, 7, 7)

@@ -24,10 +24,9 @@ RUN = 4
 PAIR = 2
 QUADS = 4
 
-X_LOADS = [(0, 0, 512), (1, 0, 256), (1, 256, 256), (0, 512, 512), (1, 512, 256), (1, 768, 128), (1, 896, 128)]
-X_PIECE = 256
-
-SHARE, SHARE_LARGE, SHARE_EVEN = 5, 6, 4
+LOADS = [("c", 0, 0, T), ("c", 1, 0, T), ("wc", 1, 0, R), ("wx", 0, 0, R), ("wx", 1, 0, R),
+         ("x", 0, 0, 512), ("x", 1, 0, 256), ("x", 1, 256, 256), ("x", 0, 512, 256), ("x", 1, 512, 256), ("x", 0, 768, 256), ("x", 1, 768, 256)]
+STEP = 32
 
 
 def tile_mix_bilin_fm_pl_none_kernel(tc, x, wx, c, wc, w_words, w_scales, out_0, out_1, out_2):
@@ -37,125 +36,104 @@ def tile_mix_bilin_fm_pl_none_kernel(tc, x, wx, c, wc, w_words, w_scales, out_0,
         ps = ctx.enter_context(tc.psum_pool(name="ps", bufs=1))
         ctx.enter_context(tc.manual_schedule())
 
-        raw, rounded, words, planes = {}, {}, {}, {}
-        x_piece_of = {}
+        raw, landed_in, rounded, words, planes = {}, {}, {}, {}, {}
+        for name, width in (("wc", R), ("c", T), ("wx", R), ("x", T)):
+            for g in range(PASSES):
+                rounded[name, g] = sb.tile([P, PACK * width], BF16, name="rounded_%s_%d" % (name, g), align_bytes=64)
+                words[name, g] = sb.tile([P, width], U32, name="words_%s_%d" % (name, g), align_bytes=64)
+                planes[name, g] = sb.tile([P, width], U8, name="plane_%s_%d" % (name, g), align_bytes=64)
 
-        def declare(piece, values):
-            label = "%s_%d_%d" % piece
-            width = values.shape[2]
-            raw[piece] = values
-            rounded[piece] = sb.tile([P, PACK * width], BF16, name="rounded_" + label, align_bytes=64)
-            words[piece] = sb.tile([P, width], U32, name="words_" + label, align_bytes=64)
-            planes[piece] = sb.tile([P, width], U8, name="plane_" + label, align_bytes=64)
-
-        def load(name, src, g, t0, width, piece_width):
+        def load(name, src, g, t0, width):
             landed = sb.tile([P, PACK, width], F32, name="raw_%s_%d_%d" % (name, g, t0))
             rows = src[g * K_PASS : (g + 1) * K_PASS, t0 : t0 + width]
             nc.sync.dma_start(out=landed[:], in_=rows.rearrange("(p j) w -> p j w", j=PACK))
-            for p0 in range(0, width, piece_width):
-                declare((name, g, t0 + p0), landed[:, :, p0 : p0 + piece_width])
+            raw[name, g] = landed
+            for t in range(t0, t0 + width, STEP):
+                landed_in[name, g, t // STEP] = (landed, t0)
 
         w_plane_raw = sb.tile([P, M], U8, name="w_plane_raw", align_bytes=64)
         nc.vector.memset(w_plane_raw[:].bitcast(I32), 0)
 
-        wc_raw = sb.tile([P, PASSES, PACK, R], F32, name="wc_raw")
-        nc.sync.dma_start(
-            out=wc_raw[:].rearrange("p g j r -> p g (j r)"),
-            in_=wc.rearrange("(g p j) r -> p g (j r)", g=PASSES, j=PACK),
-        )
-        for g in range(PASSES):
-            declare(("wc", g, 0), wc_raw[:, g])
+        load("wc", wc, 0, 0, R)
 
         w_words_raw = sb.tile([P, 2 * M], U8, name="w_words_raw", align_bytes=64)
-        nc.scalar.dma_start(out=w_words_raw[:].bitcast(I32), in_=w_words[0].bitcast(I32))
+        nc.sync.dma_start(out=w_words_raw[:].bitcast(I32), in_=w_words[0].bitcast(I32))
         for quad in range(QUADS):
-            nc.scalar.dma_start(
+            nc.sync.dma_start(
                 out=w_plane_raw[32 * quad : 32 * quad + 4, :].bitcast(I32),
                 in_=w_scales[0, 4 * quad : 4 * quad + 4, :].bitcast(I32),
             )
 
-        for g in range(PASSES):
-            load("c", c, g, 0, T, HALF)
-        for g in range(PASSES):
-            load("wx", wx, g, 0, R, R)
-        for g, t0, width in X_LOADS:
-            piece_width = min(width, X_PIECE)
-            load("x", x, g, t0, width, piece_width)
-            for t in range(t0, t0 + width, CHUNK):
-                x_piece_of[g, t // CHUNK] = t0 + (t - t0) // piece_width * piece_width
+        sources = {"wc": wc, "c": c, "wx": wx, "x": x}
+        for name, g, t0, width in LOADS:
+            load(name, sources[name], g, t0, width)
 
-        def round_weight(piece):
-            dst = rounded[piece][:].rearrange("p (i m j) -> p m j i", i=PACK, j=PACK)
-            src = raw[piece].rearrange("p j (m i) -> p m j i", i=PACK)
-            nc.vector.tensor_copy(out=dst[:, :, :, 0:2], in_=src[:, :, :, 0:2])
-            nc.scalar.copy(out=dst[:, :, :, 2:4], in_=src[:, :, :, 2:4])
+        def round_weight(engine_copy, name, g, first, m0=0, m1=P):
+            dst = rounded[name, g][:].rearrange("p (i m j) -> p m j i", i=PACK, j=PACK)
+            src = raw[name, g][:].rearrange("p j (m i) -> p m j i", i=PACK)
+            engine_copy(out=dst[:, m0:m1, :, first : first + PAIR], in_=src[:, m0:m1, :, first : first + PAIR])
 
-        def run_views(piece):
-            dst = rounded[piece][:].rearrange("p (c i j) -> p c j i", i=PAIR, j=PACK)
-            return dst, raw[piece].rearrange("p j (c i) -> p c j i", i=PAIR)
+        def round_columns(engine_copy, name, g, t0, t1):
+            landed, first = landed_in[name, g, t0 // STEP]
+            dst = rounded[name, g][:, PACK * t0 : PACK * t1].rearrange("p (c i j) -> p c j i", i=PAIR, j=PACK)
+            src = landed[:, :, t0 - first : t1 - first].rearrange("p j (c i) -> p c j i", i=PAIR)
+            engine_copy(out=dst, in_=src)
 
-        def round_on_vector(piece, eighths):
-            dst, src = run_views(piece)
-            cut = dst.shape[1] * eighths // 8
-            nc.vector.tensor_copy(out=dst[:, :cut], in_=src[:, :cut])
+        def quantise(name, g, t0, t1):
+            fmt = E5M2 if name == "c" else E4M3
+            nc.vector.quantize_mx(
+                out=words[name, g][:, t0:t1].bitcast(fmt),
+                scales=planes[name, g][:, t0:t1],
+                in_=rounded[name, g][:, PACK * t0 : PACK * t1],
+            )
 
-        def round_on_scalar(piece, eighths):
-            dst, src = run_views(piece)
-            cut = dst.shape[1] * eighths // 8
-            nc.scalar.copy(out=dst[:, cut:], in_=src[:, cut:])
-
-        def round_shared(piece):
-            round_on_vector(piece, SHARE)
-            round_on_scalar(piece, SHARE)
-
-        def quantise(piece):
-            fmt = E5M2 if piece[0] == "c" else E4M3
-            nc.vector.quantize_mx(out=words[piece][:].bitcast(fmt), scales=planes[piece][:], in_=rounded[piece][:])
+        on_vector, on_scalar = nc.vector.tensor_copy, nc.scalar.copy
 
         pc_bank, px_bank, y_bank = {}, {}, {}
         pc_sb = sb.tile([P, T // RUN, PACK, RUN], F32, name="pc_sb")
         y_sb = sb.tile([P, PACK, T], F32, name="y_sb")
+        y_rounded = sb.tile([P, PACK * T], BF16, name="y_rounded", align_bytes=64)
         y_words = sb.tile([P, T], U32, name="y_words", align_bytes=64)
         y_plane = sb.tile([P, T // PACK], U8, name="y_plane", align_bytes=64)
-        h_rounded, h_words, h_plane, y_rounded = {}, {}, {}, {}
+        h_rounded, h_words, h_plane = {}, {}, {}
         w_words_dealt = sb.tile([P, 2 * M], U8, name="w_words_dealt", align_bytes=64)
         w_plane_dealt = sb.tile([P, M], U8, name="w_plane_dealt", align_bytes=64)
 
-        def project_c(half):
+        def project_c(g, half):
             for i in range(PACK):
-                pc_bank[half, i] = ps.tile([P, HALF], F32, name="pc_%d_%d" % (half, i), tag="bank%d" % (PACK * half + i))
+                if g == 0:
+                    pc_bank[half, i] = ps.tile([P, HALF], F32, name="pc_%d_%d" % (half, i), tag="bank%d" % (PACK * half + i))
                 dealt = slice(i * P, (i + 1) * P)
-                for g in range(PASSES):
-                    nc.tensor.matmul_mx(
-                        out=pc_bank[half, i][:],
-                        lhsT=words["wc", g, 0][:, dealt].bitcast(E4M3),
-                        lhsT_scale=planes["wc", g, 0][:, dealt],
-                        rhs=words["c", g, half * HALF][:].bitcast(E5M2),
-                        rhs_scale=planes["c", g, half * HALF][:],
-                        start=(g == 0),
-                        stop=(g == PASSES - 1),
-                    )
+                cols = slice(half * HALF, (half + 1) * HALF)
+                nc.tensor.matmul_mx(
+                    out=pc_bank[half, i][:],
+                    lhsT=words["wc", g][:, dealt].bitcast(E4M3),
+                    lhsT_scale=planes["wc", g][:, dealt],
+                    rhs=words["c", g][:, cols].bitcast(E5M2),
+                    rhs_scale=planes["c", g][:, cols],
+                    start=(g == 0),
+                    stop=(g == PASSES - 1),
+                )
 
-        def empty_pc(half, i):
+        def empty_pc(engine_copy, half, i):
             runs = slice(half * HALF // RUN, (half + 1) * HALF // RUN)
-            nc.scalar.copy(out=pc_sb[:, runs, i, :], in_=pc_bank[half, i][:].rearrange("p (c u) -> p c u", u=RUN))
+            engine_copy(out=pc_sb[:, runs, i, :], in_=pc_bank[half, i][:].rearrange("p (c u) -> p c u", u=RUN))
 
-        def project_x(e):
-            px_bank[e] = ps.tile([P, PACK, CHUNK], F32, name="px_%d" % e, tag="bank%d" % (e % PACK))
+        def project_x(g, e):
+            if g == 0:
+                px_bank[e] = ps.tile([P, PACK, CHUNK], F32, name="px_%d" % e, tag="bank%d" % e)
+            cols = slice(e * CHUNK, (e + 1) * CHUNK)
             for i in range(PACK):
                 dealt = slice(i * P, (i + 1) * P)
-                for g in range(PASSES):
-                    p0 = x_piece_of[g, e]
-                    cols = slice(e * CHUNK - p0, (e + 1) * CHUNK - p0)
-                    nc.tensor.matmul_mx(
-                        out=px_bank[e][:, i, :],
-                        lhsT=words["wx", g, 0][:, dealt].bitcast(E4M3),
-                        lhsT_scale=planes["wx", g, 0][:, dealt],
-                        rhs=words["x", g, p0][:, cols].bitcast(E4M3),
-                        rhs_scale=planes["x", g, p0][:, cols],
-                        start=(g == 0),
-                        stop=(g == PASSES - 1),
-                    )
+                nc.tensor.matmul_mx(
+                    out=px_bank[e][:, i, :],
+                    lhsT=words["wx", g][:, dealt].bitcast(E4M3),
+                    lhsT_scale=planes["wx", g][:, dealt],
+                    rhs=words["x", g][:, cols].bitcast(E4M3),
+                    rhs_scale=planes["x", g][:, cols],
+                    start=(g == 0 and i == 0),
+                    stop=(g == PASSES - 1 and i == PACK - 1),
+                )
 
         def multiply(e):
             h_rounded[e] = sb.tile([P, PACK * CHUNK], BF16, name="h_rounded_%d" % e, align_bytes=64)
@@ -166,14 +144,11 @@ def tile_mix_bilin_fm_pl_none_kernel(tc, x, wx, c, wc, w_words, w_scales, out_0,
                 op=mybir.AluOpType.mult,
             )
 
-        def project_h(e):
-            h_words[e] = sb.tile([P, CHUNK], U32, name="h_words_%d" % e, align_bytes=64)
-            h_plane[e] = sb.tile([P, CHUNK], U8, name="h_plane_%d" % e, align_bytes=64)
-            nc.vector.quantize_mx(out=h_words[e][:].bitcast(E4M3), scales=h_plane[e][:], in_=h_rounded[e][:])
-            y_bank[e] = ps.tile([P, PACK, CHUNK], F32, name="y_%d" % e, tag="bank%d" % (PACK + e % PACK))
+        def project_h(e, bank):
+            y_bank[e, bank] = ps.tile([P, PACK, CHUNK], F32, name="y_%d_%d" % (e, bank), tag="bank%d" % bank)
             for i in range(PACK):
                 nc.tensor.matmul_mx(
-                    out=y_bank[e][:, i, :],
+                    out=y_bank[e, bank][:, i, :],
                     lhsT=w_words_dealt[:, 2 * i * P : 2 * (i + 1) * P].bitcast(E2M1),
                     lhsT_scale=w_plane_dealt[:, i * P : (i + 1) * P],
                     rhs=h_words[e][:].bitcast(E4M3),
@@ -181,6 +156,12 @@ def tile_mix_bilin_fm_pl_none_kernel(tc, x, wx, c, wc, w_words, w_scales, out_0,
                     start=True,
                     stop=True,
                 )
+
+        def quantise_h(e):
+            h_words[e] = sb.tile([P, CHUNK], U32, name="h_words_%d" % e, align_bytes=64)
+            h_plane[e] = sb.tile([P, CHUNK], U8, name="h_plane_%d" % e, align_bytes=64)
+            nc.vector.quantize_mx(out=h_words[e][:].bitcast(E4M3), scales=h_plane[e][:], in_=h_rounded[e][:])
+            project_h(e, e)
 
         def deal_w():
             nc.vector.tensor_copy(
@@ -192,135 +173,162 @@ def tile_mix_bilin_fm_pl_none_kernel(tc, x, wx, c, wc, w_words, w_scales, out_0,
                 in_=w_plane_raw[:].rearrange("p (m i) -> p i m", i=PACK),
             )
 
-        def copy_y(e):
-            nc.scalar.copy(out=y_sb[:, :, e * CHUNK : (e + 1) * CHUNK], in_=y_bank[e][:])
+        def copy_y(engine_copy, e, bank):
+            engine_copy(out=y_sb[:, :, e * CHUNK : (e + 1) * CHUNK], in_=y_bank[e, bank][:])
 
-        def round_y_from_psum(e):
-            y_rounded[e] = sb.tile([P, PACK * CHUNK], BF16, name="y_rounded_%d" % e, align_bytes=64)
-            nc.scalar.copy(out=y_rounded[e][:].rearrange("p (t i) -> p t i", i=PACK), in_=y_bank[e][:].rearrange("p i t -> p t i"))
+        def round_y_from_psum(engine_copy, e, bank):
+            dst = y_rounded[:, PACK * e * CHUNK : PACK * (e + 1) * CHUNK]
+            engine_copy(out=dst.rearrange("p (t i) -> p t i", i=PACK), in_=y_bank[e, bank][:].rearrange("p i t -> p t i"))
 
-        def round_y_from_sbuf(e):
-            y_rounded[e] = sb.tile([P, PACK * CHUNK], BF16, name="y_rounded_%d" % e, align_bytes=64)
-            nc.vector.tensor_copy(
-                out=y_rounded[e][:].rearrange("p (c u i) -> p c i u", u=PAIR, i=PACK),
-                in_=y_sb[:, :, e * CHUNK : (e + 1) * CHUNK].rearrange("p i (c u) -> p c i u", u=PAIR),
+        def round_y_from_sbuf(engine_copy, first, last):
+            t0, t1 = first * CHUNK, (last + 1) * CHUNK
+            engine_copy(
+                out=y_rounded[:, PACK * t0 : PACK * t1].rearrange("p (c u i) -> p c i u", u=PAIR, i=PACK),
+                in_=y_sb[:, :, t0:t1].rearrange("p i (c u) -> p c i u", u=PAIR),
             )
 
-        def quantise_y(e):
-            cols = slice(e * CHUNK, (e + 1) * CHUNK)
-            k, first = divmod(e * CHUNK, T // PACK)
-            scales = y_plane[4 * k :, first : first + CHUNK]
-            nc.vector.quantize_mx(out=y_words[:, cols].bitcast(E4M3), scales=scales, in_=y_rounded[e][:])
+        def quantise_y(first, last):
+            t0, t1 = first * CHUNK, (last + 1) * CHUNK
+            k, column = divmod(t0, T // PACK)
+            nc.vector.quantize_mx(
+                out=y_words[:, t0:t1].bitcast(E4M3),
+                scales=y_plane[4 * k :, column : column + t1 - t0],
+                in_=y_rounded[:, PACK * t0 : PACK * t1],
+            )
 
-        def store_values(first, last):
+        def store_values(queue, first, last):
             cols = slice(first * CHUNK, (last + 1) * CHUNK)
-            nc.sync.dma_start(out=out_0.rearrange("(p i) t -> p i t", i=PACK)[:, :, cols], in_=y_sb[:, :, cols])
+            queue.dma_start(out=out_0.rearrange("(p i) t -> p i t", i=PACK)[:, :, cols], in_=y_sb[:, :, cols])
 
         def store_words(queue, first, last):
             cols = slice(first * CHUNK, (last + 1) * CHUNK)
             queue.dma_start(out=out_1[0].rearrange("p t i -> p (t i)").bitcast(I32)[:, cols], in_=y_words[:, cols].bitcast(I32))
 
-        for g in range(PASSES):
-            round_weight(("wc", g, 0))
-        for g in range(PASSES):
-            quantise(("wc", g, 0))
-        for t0 in (0, HALF):
-            round_shared(("c", 0, t0))
-        for t0 in (0, HALF):
-            quantise(("c", 0, t0))
-        deal_w()
-        for t0 in (0, HALF):
-            round_shared(("c", 1, t0))
-        quantise(("c", 1, 0))
-        project_c(0)
-        round_weight(("wx", 0, 0))
-        quantise(("c", 1, HALF))
-        project_c(1)
-        quantise(("wx", 0, 0))
-        empty_pc(0, 0)
-        round_weight(("wx", 1, 0))
-        quantise(("wx", 1, 0))
-        empty_pc(0, 1)
-        empty_pc(0, 2)
-
-        round_shared(("x", 0, 0))
-        round_shared(("x", 0, 256))
-        quantise(("x", 0, 0))
-        empty_pc(0, 3)
-        round_shared(("x", 1, 0))
-        quantise(("x", 0, 256))
-        quantise(("x", 1, 0))
-        project_x(0)
-        project_x(1)
-        empty_pc(1, 0)
-        round_shared(("x", 1, 256))
-        quantise(("x", 1, 256))
-        project_x(2)
-        project_x(3)
-        for i in range(1, PACK):
-            empty_pc(1, i)
-        multiply(0)
-        for e in range(3):
-            multiply(e + 1)
-            project_h(e)
-
-        round_on_scalar(("x", 0, 512), 0)
-        round_on_scalar(("x", 0, 768), SHARE_EVEN)
-        round_on_scalar(("x", 1, 512), SHARE_LARGE)
-        round_on_vector(("x", 1, 512), SHARE_LARGE)
-        project_h(3)
-        quantise(("x", 0, 512))
-        quantise(("x", 1, 512))
-        project_x(4)
-        project_x(5)
-        round_on_vector(("x", 1, 768), 8)
-        round_on_vector(("x", 0, 768), SHARE_EVEN)
-        quantise(("x", 1, 768))
-        round_on_vector(("x", 1, 896), 8)
-        quantise(("x", 0, 768))
-        quantise(("x", 1, 896))
-        project_x(6)
-        project_x(7)
-        for e in range(4):
-            copy_y(e)
-        store_values(0, 1)
-        store_values(2, 3)
-        for e in range(4):
-            round_y_from_psum(e)
-
-        multiply(4)
-        multiply(5)
-        project_h(4)
-        quantise_y(0)
-        quantise_y(1)
-        project_h(5)
-        multiply(6)
-        quantise_y(2)
-        quantise_y(3)
-        store_words(nc.sync, 0, 3)
-        project_h(6)
-        multiply(7)
-        copy_y(4)
-        round_y_from_sbuf(4)
-        project_h(7)
-        copy_y(5)
-        store_values(4, 5)
-        round_y_from_sbuf(5)
-        quantise_y(4)
-        quantise_y(5)
-        copy_y(6)
-        store_values(6, 6)
-        round_y_from_psum(6)
-        quantise_y(6)
-        store_words(nc.sync, 4, 6)
-        round_y_from_psum(7)
-        copy_y(7)
-        quantise_y(7)
-
-        store_values(7, 7)
-        for quad in range(QUADS):
-            nc.scalar.dma_start(
+        def store_scales(queue, quad):
+            queue.dma_start(
                 out=out_2[0, 4 * quad : 4 * quad + 4, :].bitcast(I32).rearrange("s (k c) -> k s c", k=PACK),
                 in_=y_plane[32 * quad : 32 * quad + 16, :].bitcast(I32),
             )
-        store_words(nc.scalar, 7, 7)
+
+        round_weight(on_vector, "wc", 0, 0)
+        round_weight(on_scalar, "wc", 0, 2)
+        quantise("wc", 0, 0, R)
+        deal_w()
+        for g in range(PASSES):
+            for t0 in (0, HALF):
+                round_columns(on_vector, "c", g, t0, t0 + 320)
+                round_columns(on_scalar, "c", g, t0 + 320, t0 + HALF)
+            for half in range(2):
+                quantise("c", g, half * HALF, (half + 1) * HALF)
+                if g == 0:
+                    project_c(0, half)
+        round_weight(on_vector, "wc", 1, 0)
+        round_weight(on_vector, "wc", 1, 2, 0, 48)
+        round_weight(on_scalar, "wc", 1, 2, 48, P)
+        quantise("wc", 1, 0, R)
+        for half in range(2):
+            project_c(1, half)
+        for half in range(2):
+            for i in range(PACK):
+                if (half, i) != (1, 3):
+                    empty_pc(on_scalar, half, i)
+        round_weight(on_vector, "wx", 0, 0)
+        round_weight(on_vector, "wx", 0, 2)
+        quantise("wx", 0, 0, R)
+        round_weight(on_vector, "wx", 1, 0)
+        round_weight(on_vector, "wx", 1, 2)
+        empty_pc(on_vector, 1, 3)
+        quantise("wx", 1, 0, R)
+
+        round_columns(on_vector, "x", 0, 0, 128)
+        round_columns(on_scalar, "x", 0, 256, 512)
+        round_columns(on_vector, "x", 0, 128, 256)
+        quantise("x", 0, 0, 128)
+        project_x(0, 0)
+        quantise("x", 0, 128, 256)
+        project_x(0, 1)
+        round_columns(on_vector, "x", 1, 0, 128)
+        round_columns(on_scalar, "x", 1, 128, 256)
+        quantise("x", 0, 256, 512)
+        quantise("x", 1, 0, 128)
+        project_x(1, 0)
+        quantise("x", 1, 128, 256)
+        project_x(1, 1)
+        project_x(0, 2)
+        project_x(0, 3)
+        round_columns(on_vector, "x", 1, 256, 384)
+        round_columns(on_scalar, "x", 1, 384, 512)
+        multiply(0)
+        quantise("x", 1, 256, 384)
+        project_x(1, 2)
+        multiply(1)
+        quantise("x", 1, 384, 512)
+        project_x(1, 3)
+        round_columns(on_scalar, "x", 0, 512, 768)
+        quantise_h(0)
+        quantise_h(1)
+        multiply(2)
+        quantise("x", 0, 512, 768)
+        project_x(0, 4)
+        round_columns(on_scalar, "x", 1, 512, 640)
+        multiply(3)
+        copy_y(on_scalar, 0, 0)
+        copy_y(on_scalar, 1, 1)
+        store_values(nc.sync, 0, 1)
+        quantise_h(2)
+        quantise("x", 1, 512, 640)
+        project_x(1, 4)
+        project_x(0, 5)
+        round_columns(on_vector, "x", 1, 640, 768)
+        quantise_h(3)
+        round_columns(on_vector, "x", 0, 768, 896)
+        round_columns(on_scalar, "x", 0, 896, 1024)
+        quantise("x", 1, 640, 768)
+        project_x(1, 5)
+        multiply(4)
+        quantise("x", 0, 768, 1024)
+        project_x(0, 6)
+        copy_y(on_scalar, 2, 2)
+        round_columns(on_scalar, "x", 1, 768, 896)
+        copy_y(on_scalar, 3, 3)
+        store_values(nc.sync, 2, 3)
+        quantise_h(4)
+        project_x(0, 7)
+        multiply(5)
+        quantise("x", 1, 768, 896)
+        project_x(1, 6)
+        round_columns(on_vector, "x", 1, 896, 1024)
+        quantise_h(5)
+        round_y_from_sbuf(on_vector, 0, 0)
+        quantise("x", 1, 896, 1024)
+        project_x(1, 7)
+        round_y_from_psum(on_scalar, 1, 1)
+        copy_y(on_scalar, 4, 4)
+        copy_y(on_scalar, 5, 5)
+        store_values(nc.sync, 4, 5)
+        multiply(6)
+        round_y_from_sbuf(on_vector, 2, 2)
+        quantise_h(6)
+        multiply(7)
+        round_y_from_psum(on_scalar, 3, 3)
+        quantise_y(0, 1)
+        quantise_h(7)
+        project_h(7, 0)
+        round_y_from_psum(on_scalar, 4, 4)
+        quantise_y(2, 3)
+        store_words(nc.sync, 0, 3)
+        round_y_from_sbuf(on_vector, 5, 5)
+        copy_y(on_scalar, 6, 6)
+        copy_y(on_scalar, 7, 7)
+        store_values(nc.sync, 6, 7)
+        round_y_from_sbuf(on_vector, 6, 6)
+        quantise_y(4, 5)
+        store_words(nc.sync, 4, 5)
+        round_y_from_psum(on_vector, 7, 0)
+        quantise_y(6, 6)
+        quantise_y(7, 7)
+        store_scales(nc.scalar, 0)
+        store_words(nc.sync, 6, 7)
+        store_scales(nc.scalar, 1)
+        store_scales(nc.sync, 2)
+        store_scales(nc.sync, 3)

@@ -163,6 +163,26 @@ def tile_mix_bilin_fm_pl_none_kernel(tc, x, wx, c, wc, w_words, w_scales, out_0,
             nc.vector.quantize_mx(out=h_words[e][:].bitcast(E4M3), scales=h_plane[e][:], in_=h_rounded[e][:])
             project_h(e, e)
 
+        def quantise_last_h(e, spare):
+            h_words[e] = sb.tile([P, CHUNK], U32, name="h_words_%d" % e, align_bytes=64)
+            h_plane[e] = sb.tile([P, CHUNK], U8, name="h_plane_%d" % e, align_bytes=64)
+            nc.vector.quantize_mx(out=h_words[e][:].bitcast(E4M3), scales=h_plane[e][:], in_=h_rounded[e][:])
+            for first, bank in ((0, e), (PAIR, spare)):
+                y_bank[e, bank] = ps.tile([P, PAIR, CHUNK], F32, name="y_%d_%d" % (e, bank), tag="bank%d" % bank)
+                for i in range(first, first + PAIR):
+                    nc.tensor.matmul_mx(
+                        out=y_bank[e, bank][:, i - first, :],
+                        lhsT=w_words_dealt[:, 2 * i * P : 2 * (i + 1) * P].bitcast(E2M1),
+                        lhsT_scale=w_plane_dealt[:, i * P : (i + 1) * P],
+                        rhs=h_words[e][:].bitcast(E4M3),
+                        rhs_scale=h_plane[e][:],
+                        start=True,
+                        stop=True,
+                    )
+
+        def copy_y_pair(engine_copy, e, bank, first):
+            engine_copy(out=y_sb[:, first : first + PAIR, e * CHUNK : (e + 1) * CHUNK], in_=y_bank[e, bank][:])
+
         def deal_w():
             nc.vector.tensor_copy(
                 out=w_words_dealt[:].rearrange("p (i m b) -> p i m b", i=PACK, b=2),
@@ -228,16 +248,15 @@ def tile_mix_bilin_fm_pl_none_kernel(tc, x, wx, c, wc, w_words, w_scales, out_0,
         quantise("wc", 1, 0, R)
         for half in range(2):
             project_c(1, half)
-        for half in range(2):
-            for i in range(PACK):
-                if (half, i) != (1, 3):
-                    empty_pc(on_scalar, half, i)
+        for i in range(PACK):
+            empty_pc(on_scalar, 0, i)
         round_weight(on_vector, "wx", 0, 0)
         round_weight(on_vector, "wx", 0, 2)
         quantise("wx", 0, 0, R)
         round_weight(on_vector, "wx", 1, 0)
         round_weight(on_vector, "wx", 1, 2)
-        empty_pc(on_vector, 1, 3)
+        empty_pc(on_scalar, 1, 0)
+        empty_pc(on_scalar, 1, 1)
         quantise("wx", 1, 0, R)
 
         round_columns(on_vector, "x", 0, 0, 128)
@@ -252,81 +271,82 @@ def tile_mix_bilin_fm_pl_none_kernel(tc, x, wx, c, wc, w_words, w_scales, out_0,
         quantise("x", 0, 256, 512)
         quantise("x", 1, 0, 128)
         project_x(1, 0)
+        empty_pc(on_scalar, 1, 2)
         quantise("x", 1, 128, 256)
         project_x(1, 1)
         project_x(0, 2)
         project_x(0, 3)
         round_columns(on_vector, "x", 1, 256, 384)
         round_columns(on_scalar, "x", 1, 384, 512)
+        empty_pc(on_scalar, 1, 3)
         multiply(0)
         quantise("x", 1, 256, 384)
         project_x(1, 2)
         multiply(1)
-        quantise("x", 1, 384, 512)
-        project_x(1, 3)
         round_columns(on_scalar, "x", 0, 512, 768)
         quantise_h(0)
+        quantise("x", 1, 384, 512)
+        project_x(1, 3)
         quantise_h(1)
         multiply(2)
+        round_columns(on_scalar, "x", 1, 512, 640)
         quantise("x", 0, 512, 768)
         project_x(0, 4)
-        round_columns(on_scalar, "x", 1, 512, 640)
-        multiply(3)
+        project_x(0, 5)
+        round_columns(on_vector, "x", 1, 640, 768)
         copy_y(on_scalar, 0, 0)
         copy_y(on_scalar, 1, 1)
         store_values(nc.sync, 0, 1)
-        quantise_h(2)
         quantise("x", 1, 512, 640)
         project_x(1, 4)
-        project_x(0, 5)
-        round_columns(on_vector, "x", 1, 640, 768)
-        quantise_h(3)
-        round_columns(on_vector, "x", 0, 768, 896)
-        round_columns(on_scalar, "x", 0, 896, 1024)
+        quantise_h(2)
         quantise("x", 1, 640, 768)
         project_x(1, 5)
+        multiply(3)
+        round_columns(on_scalar, "x", 0, 768, 1024)
+        round_y_from_sbuf(on_vector, 0, 0)
+        quantise_h(3)
         multiply(4)
+        round_columns(on_scalar, "x", 1, 768, 896)
+        round_columns(on_scalar, "x", 1, 896, 1024)
         quantise("x", 0, 768, 1024)
         project_x(0, 6)
-        copy_y(on_scalar, 2, 2)
-        round_columns(on_scalar, "x", 1, 768, 896)
-        copy_y(on_scalar, 3, 3)
-        store_values(nc.sync, 2, 3)
         quantise_h(4)
-        project_x(0, 7)
-        multiply(5)
         quantise("x", 1, 768, 896)
         project_x(1, 6)
-        round_columns(on_vector, "x", 1, 896, 1024)
-        quantise_h(5)
-        round_y_from_sbuf(on_vector, 0, 0)
+        project_x(0, 7)
+        multiply(5)
         quantise("x", 1, 896, 1024)
         project_x(1, 7)
-        round_y_from_psum(on_scalar, 1, 1)
-        copy_y(on_scalar, 4, 4)
-        copy_y(on_scalar, 5, 5)
-        store_values(nc.sync, 4, 5)
+        copy_y(on_scalar, 2, 2)
+        copy_y(on_scalar, 3, 3)
+        store_values(nc.sync, 2, 3)
+        round_y_from_sbuf(on_vector, 1, 1)
+        quantise_h(5)
         multiply(6)
-        round_y_from_sbuf(on_vector, 2, 2)
+        round_y_from_psum(on_scalar, 2, 2)
+        copy_y(on_scalar, 4, 4)
+        quantise_y(0, 1)
+        store_words(nc.sync, 0, 1)
         quantise_h(6)
         multiply(7)
-        round_y_from_psum(on_scalar, 3, 3)
-        quantise_y(0, 1)
-        quantise_h(7)
-        project_h(7, 0)
+        copy_y(on_scalar, 5, 5)
+        store_values(nc.sync, 4, 5)
+        round_y_from_sbuf(on_vector, 3, 3)
+        quantise_last_h(7, 0)
         round_y_from_psum(on_scalar, 4, 4)
-        quantise_y(2, 3)
-        store_words(nc.sync, 0, 3)
         round_y_from_sbuf(on_vector, 5, 5)
-        copy_y(on_scalar, 6, 6)
-        copy_y(on_scalar, 7, 7)
-        store_values(nc.sync, 6, 7)
-        round_y_from_sbuf(on_vector, 6, 6)
+        quantise_y(2, 3)
+        store_words(nc.sync, 2, 3)
         quantise_y(4, 5)
         store_words(nc.sync, 4, 5)
-        round_y_from_psum(on_vector, 7, 0)
-        quantise_y(6, 6)
-        quantise_y(7, 7)
+        copy_y(on_scalar, 6, 6)
+        round_y_from_psum(on_scalar, 6, 6)
+        copy_y_pair(on_vector, 7, 7, 0)
+        copy_y_pair(on_scalar, 7, 0, 2)
+        store_values(nc.sync, 6, 7)
+        round_y_from_sbuf(on_vector, 7, 7)
+        quantise_y(6, 7)
         store_scales(nc.scalar, 0)
         store_words(nc.sync, 6, 7)
         store_scales(nc.scalar, 1)

@@ -90,7 +90,7 @@ def tile_mix_bilin_fm_pl_none_kernel(tc, x, wx, c, wc, w_words, w_scales, out_0,
         on_vector, on_scalar = nc.vector.tensor_copy, nc.scalar.copy
 
         pc_bank, px_bank, y_bank = {}, {}, {}
-        pc_sb = sb.tile([P, T // RUN, PACK, RUN], F32, name="pc_sb")
+        pc_sb = sb.tile([P, PACK, T], F32, name="pc_sb")
         y_sb = sb.tile([P, PACK, T], F32, name="y_sb")
         y_rounded = sb.tile([P, PACK * T], BF16, name="y_rounded", align_bytes=64)
         y_words = sb.tile([P, T], U32, name="y_words", align_bytes=64)
@@ -99,8 +99,8 @@ def tile_mix_bilin_fm_pl_none_kernel(tc, x, wx, c, wc, w_words, w_scales, out_0,
         w_words_dealt = sb.tile([P, 2 * M], U8, name="w_words_dealt", align_bytes=64)
         w_plane_dealt = sb.tile([P, M], U8, name="w_plane_dealt", align_bytes=64)
 
-        def project_c(g, half):
-            for i in range(PACK):
+        def project_c(g, half, first=0, count=PACK):
+            for i in range(first, first + count):
                 if g == 0:
                     pc_bank[half, i] = ps.tile([P, HALF], F32, name="pc_%d_%d" % (half, i), tag="bank%d" % (PACK * half + i))
                 dealt = slice(i * P, (i + 1) * P)
@@ -116,8 +116,7 @@ def tile_mix_bilin_fm_pl_none_kernel(tc, x, wx, c, wc, w_words, w_scales, out_0,
                 )
 
         def empty_pc(engine_copy, half, i):
-            runs = slice(half * HALF // RUN, (half + 1) * HALF // RUN)
-            engine_copy(out=pc_sb[:, runs, i, :], in_=pc_bank[half, i][:].rearrange("p (c u) -> p c u", u=RUN))
+            engine_copy(out=pc_sb[:, i, half * HALF : (half + 1) * HALF], in_=pc_bank[half, i][:])
 
         def project_x(g, e):
             if g == 0:
@@ -140,7 +139,7 @@ def tile_mix_bilin_fm_pl_none_kernel(tc, x, wx, c, wc, w_words, w_scales, out_0,
             nc.vector.tensor_tensor(
                 out=h_rounded[e][:].rearrange("p (c u i) -> p c i u", u=RUN, i=PACK),
                 in0=px_bank[e][:].rearrange("p i (c u) -> p c i u", u=RUN),
-                in1=pc_sb[:, e * CHUNK // RUN : (e + 1) * CHUNK // RUN],
+                in1=pc_sb[:, :, e * CHUNK : (e + 1) * CHUNK].rearrange("p i (c u) -> p c i u", u=RUN),
                 op=mybir.AluOpType.mult,
             )
 
@@ -243,41 +242,45 @@ def tile_mix_bilin_fm_pl_none_kernel(tc, x, wx, c, wc, w_words, w_scales, out_0,
                 if g == 0:
                     project_c(0, half)
         round_weight(on_vector, "wc", 1, 0)
-        round_weight(on_vector, "wc", 1, 2, 0, 48)
-        round_weight(on_scalar, "wc", 1, 2, 48, P)
-        quantise("wc", 1, 0, R)
+        round_weight(on_scalar, "wc", 1, 2)
+        quantise("wc", 1, 0, 256)
         for half in range(2):
-            project_c(1, half)
-        for i in range(PACK):
-            empty_pc(on_scalar, 0, i)
+            project_c(1, half, 0, PAIR)
         round_weight(on_vector, "wx", 0, 0)
-        round_weight(on_vector, "wx", 0, 2)
+        round_weight(on_scalar, "wx", 0, 2)
+        empty_pc(on_vector, 0, 0)
+        empty_pc(on_scalar, 0, 1)
         quantise("wx", 0, 0, R)
         round_weight(on_vector, "wx", 1, 0)
-        round_weight(on_vector, "wx", 1, 2)
+        round_weight(on_scalar, "wx", 1, 2)
+        quantise("wc", 1, 256, R)
+        for half in range(2):
+            project_c(1, half, PAIR, PAIR)
+        empty_pc(on_vector, 1, 1)
         empty_pc(on_scalar, 1, 0)
-        empty_pc(on_scalar, 1, 1)
         quantise("wx", 1, 0, R)
-
+        empty_pc(on_scalar, 0, 2)
         round_columns(on_vector, "x", 0, 0, 128)
-        round_columns(on_scalar, "x", 0, 256, 512)
         round_columns(on_vector, "x", 0, 128, 256)
+        round_columns(on_scalar, "x", 0, 256, 384)
         quantise("x", 0, 0, 128)
         project_x(0, 0)
+        round_columns(on_vector, "x", 0, 384, 512)
         quantise("x", 0, 128, 256)
         project_x(0, 1)
+        empty_pc(on_scalar, 0, 3)
+        empty_pc(on_scalar, 1, 2)
         round_columns(on_vector, "x", 1, 0, 128)
-        round_columns(on_scalar, "x", 1, 128, 256)
-        quantise("x", 0, 256, 512)
+        round_columns(on_vector, "x", 1, 128, 256)
         quantise("x", 1, 0, 128)
         project_x(1, 0)
-        empty_pc(on_scalar, 1, 2)
+        quantise("x", 0, 256, 512)
+        project_x(0, 2)
         quantise("x", 1, 128, 256)
         project_x(1, 1)
-        project_x(0, 2)
         project_x(0, 3)
-        round_columns(on_vector, "x", 1, 256, 384)
-        round_columns(on_scalar, "x", 1, 384, 512)
+        round_columns(on_scalar, "x", 1, 256, 384)
+        round_columns(on_vector, "x", 1, 384, 512)
         empty_pc(on_scalar, 1, 3)
         multiply(0)
         quantise("x", 1, 256, 384)

@@ -291,41 +291,29 @@ def tile_mix_bilin_fm_pl_none_kernel(tc, x, wx, c, wc, w_words, w_scales, out_0,
         quantise("x", 1, 384, 512)
         project_x(1, 3)
         quantise_h(1)
-        multiply(2)
-        round_columns(on_scalar, "x", 1, 512, 640)
-        quantise("x", 0, 512, 768)
-        project_x(0, 4)
-        project_x(0, 5)
-        round_columns(on_vector, "x", 1, 640, 768)
-        copy_y(on_scalar, 0, 0)
-        copy_y(on_scalar, 1, 1)
-        store_values(nc.sync, 0, 1)
-        quantise("x", 1, 512, 640)
-        project_x(1, 4)
-        quantise_h(2)
-        quantise("x", 1, 640, 768)
-        project_x(1, 5)
-        multiply(3)
-        round_columns(on_scalar, "x", 0, 768, 1024)
-        round_y_from_sbuf(on_vector, 0, 0)
-        quantise_h(3)
-        multiply(4)
-        round_columns(on_scalar, "x", 1, 768, 896)
-        round_columns(on_scalar, "x", 1, 896, 1024)
-        quantise("x", 0, 768, 1024)
-        project_x(0, 6)
-        quantise_h(4)
-        quantise("x", 1, 768, 896)
-        project_x(1, 6)
-        project_x(0, 7)
-        multiply(5)
-        quantise("x", 1, 896, 1024)
-        project_x(1, 7)
-        copy_y(on_scalar, 2, 2)
-        copy_y(on_scalar, 3, 3)
-        store_values(nc.sync, 2, 3)
-        round_y_from_sbuf(on_vector, 1, 1)
-        quantise_h(5)
+        for a in (2, 4):
+            b, na, nb = a + 1, a + 2, a + 3
+            multiply(a)
+            round_columns(on_scalar, "x", 1, na * CHUNK, nb * CHUNK)
+            quantise("x", 0, na * CHUNK, (nb + 1) * CHUNK)
+            project_x(0, na)
+            project_x(0, nb)
+            round_columns(on_vector, "x", 1, nb * CHUNK, (nb + 1) * CHUNK)
+            copy_y(on_scalar, a - 2, a - 2)
+            copy_y(on_scalar, b - 2, b - 2)
+            store_values(nc.sync, a - 2, b - 2)
+            quantise("x", 1, na * CHUNK, nb * CHUNK)
+            project_x(1, na)
+            quantise_h(a)
+            quantise("x", 1, nb * CHUNK, (nb + 1) * CHUNK)
+            project_x(1, nb)
+            multiply(b)
+            if a == 2:
+                round_columns(on_scalar, "x", 0, 768, 1024)
+            else:
+                round_y_from_psum(on_scalar, 1, 1)
+            round_y_from_sbuf(on_vector, (0, 3)[a // 4], (0, 3)[a // 4])
+            quantise_h(b)
         multiply(6)
         round_y_from_psum(on_scalar, 2, 2)
         copy_y(on_scalar, 4, 4)
@@ -335,12 +323,11 @@ def tile_mix_bilin_fm_pl_none_kernel(tc, x, wx, c, wc, w_words, w_scales, out_0,
         multiply(7)
         copy_y(on_scalar, 5, 5)
         store_values(nc.sync, 4, 5)
-        round_y_from_sbuf(on_vector, 3, 3)
+        quantise_y(2, 3)
+        store_words(nc.sync, 2, 3)
         quantise_last_h(7, 0)
         round_y_from_psum(on_scalar, 4, 4)
         round_y_from_sbuf(on_vector, 5, 5)
-        quantise_y(2, 3)
-        store_words(nc.sync, 2, 3)
         quantise_y(4, 5)
         store_words(nc.sync, 4, 5)
         copy_y(on_scalar, 6, 6)

@@ -19,14 +19,15 @@ PACK = 4
 K_PASS = P * PACK
 PASSES = K // K_PASS
 HALF = 512
+QUARTER = 256
 CHUNK = 128
 RUN = 4
 PAIR = 2
 QUADS = 4
 
-LOADS = [("c", 0, 0, T), ("c", 1, 0, T), ("wc", 1, 0, R), ("wx", 0, 0, R), ("wx", 1, 0, R),
-         ("x", 0, 0, 512), ("x", 1, 0, 256), ("x", 1, 256, 256), ("x", 0, 512, 256), ("x", 1, 512, 256), ("x", 0, 768, 256), ("x", 1, 768, 256)]
 STEP = 32
+
+X_LOADS = [(0, 0, 512), (1, 0, 256), (1, 256, 256), (0, 512, 256), (1, 512, 256), (0, 768, 256), (1, 768, 256)]
 
 
 def tile_mix_bilin_fm_pl_none_kernel(tc, x, wx, c, wc, w_words, w_scales, out_0, out_1, out_2):
@@ -36,7 +37,7 @@ def tile_mix_bilin_fm_pl_none_kernel(tc, x, wx, c, wc, w_words, w_scales, out_0,
         ps = ctx.enter_context(tc.psum_pool(name="ps", bufs=1))
         ctx.enter_context(tc.manual_schedule())
 
-        raw, landed_in, rounded, words, planes = {}, {}, {}, {}, {}
+        landed_in, rounded, words, planes = {}, {}, {}, {}
         for name, width in (("wc", R), ("c", T), ("wx", R), ("x", T)):
             for g in range(PASSES):
                 rounded[name, g] = sb.tile([P, PACK * width], BF16, name="rounded_%s_%d" % (name, g), align_bytes=64)
@@ -47,7 +48,6 @@ def tile_mix_bilin_fm_pl_none_kernel(tc, x, wx, c, wc, w_words, w_scales, out_0,
             landed = sb.tile([P, PACK, width], F32, name="raw_%s_%d_%d" % (name, g, t0))
             rows = src[g * K_PASS : (g + 1) * K_PASS, t0 : t0 + width]
             nc.sync.dma_start(out=landed[:], in_=rows.rearrange("(p j) w -> p j w", j=PACK))
-            raw[name, g] = landed
             for t in range(t0, t0 + width, STEP):
                 landed_in[name, g, t // STEP] = (landed, t0)
 
@@ -64,14 +64,20 @@ def tile_mix_bilin_fm_pl_none_kernel(tc, x, wx, c, wc, w_words, w_scales, out_0,
                 in_=w_scales[0, 4 * quad : 4 * quad + 4, :].bitcast(I32),
             )
 
-        sources = {"wc": wc, "c": c, "wx": wx, "x": x}
-        for name, g, t0, width in LOADS:
-            load(name, sources[name], g, t0, width)
+        for g in range(PASSES):
+            load("c", c, g, 0, T)
+        load("wc", wc, 1, 0, R)
+        for g in range(PASSES):
+            load("wx", wx, g, 0, R)
+        for g, t0, width in X_LOADS:
+            load("x", x, g, t0, width)
 
-        def round_weight(engine_copy, name, g, first, m0=0, m1=P):
+        on_vector, on_scalar = nc.vector.tensor_copy, nc.scalar.copy
+
+        def round_weight(engine_copy, name, g, first):
             dst = rounded[name, g][:].rearrange("p (i m j) -> p m j i", i=PACK, j=PACK)
-            src = raw[name, g][:].rearrange("p j (m i) -> p m j i", i=PACK)
-            engine_copy(out=dst[:, m0:m1, :, first : first + PAIR], in_=src[:, m0:m1, :, first : first + PAIR])
+            src = landed_in[name, g, 0][0][:].rearrange("p j (m i) -> p m j i", i=PACK)
+            engine_copy(out=dst[:, :, :, first : first + PAIR], in_=src[:, :, :, first : first + PAIR])
 
         def round_columns(engine_copy, name, g, t0, t1):
             landed, first = landed_in[name, g, t0 // STEP]
@@ -87,8 +93,6 @@ def tile_mix_bilin_fm_pl_none_kernel(tc, x, wx, c, wc, w_words, w_scales, out_0,
                 in_=rounded[name, g][:, PACK * t0 : PACK * t1],
             )
 
-        on_vector, on_scalar = nc.vector.tensor_copy, nc.scalar.copy
-
         pc_bank, px_bank, y_bank = {}, {}, {}
         pc_sb = sb.tile([P, PACK, T], F32, name="pc_sb")
         y_sb = sb.tile([P, PACK, T], F32, name="y_sb")
@@ -97,23 +101,32 @@ def tile_mix_bilin_fm_pl_none_kernel(tc, x, wx, c, wc, w_words, w_scales, out_0,
         y_plane = sb.tile([P, T // PACK], U8, name="y_plane", align_bytes=64)
         h_rounded, h_words, h_plane = {}, {}, {}
         w_words_dealt = sb.tile([P, 2 * M], U8, name="w_words_dealt", align_bytes=64)
-        w_plane_dealt = sb.tile([P, M], U8, name="w_plane_dealt", align_bytes=64)
+        w_plane_dealt = sb.tile([P, PACK, 2 * P], U8, name="w_plane_dealt", align_bytes=64)
 
-        def project_c(g, half, first=0, count=PACK):
-            for i in range(first, first + count):
-                if g == 0:
-                    pc_bank[half, i] = ps.tile([P, HALF], F32, name="pc_%d_%d" % (half, i), tag="bank%d" % (PACK * half + i))
-                dealt = slice(i * P, (i + 1) * P)
-                cols = slice(half * HALF, (half + 1) * HALF)
-                nc.tensor.matmul_mx(
-                    out=pc_bank[half, i][:],
-                    lhsT=words["wc", g][:, dealt].bitcast(E4M3),
-                    lhsT_scale=planes["wc", g][:, dealt],
-                    rhs=words["c", g][:, cols].bitcast(E5M2),
-                    rhs_scale=planes["c", g][:, cols],
-                    start=(g == 0),
-                    stop=(g == PASSES - 1),
-                )
+        def deal_w():
+            nc.vector.tensor_copy(
+                out=w_words_dealt[:].rearrange("p (i m b) -> p i m b", i=PACK, b=2),
+                in_=w_words_raw[:].rearrange("p (m i b) -> p i m b", i=PACK, b=2),
+            )
+            nc.vector.tensor_copy(
+                out=w_plane_dealt[:, :, :P],
+                in_=w_plane_raw[:].rearrange("p (m i) -> p i m", i=PACK),
+            )
+
+        def project_c(g, half, i):
+            if g == 0:
+                pc_bank[half, i] = ps.tile([P, HALF], F32, name="pc_%d_%d" % (half, i), tag="bank%d" % (PACK * half + i))
+            dealt = slice(i * P, (i + 1) * P)
+            cols = slice(half * HALF, (half + 1) * HALF)
+            nc.tensor.matmul_mx(
+                out=pc_bank[half, i][:],
+                lhsT=words["wc", g][:, dealt].bitcast(E4M3),
+                lhsT_scale=planes["wc", g][:, dealt],
+                rhs=words["c", g][:, cols].bitcast(E5M2),
+                rhs_scale=planes["c", g][:, cols],
+                start=(g == 0),
+                stop=(g == PASSES - 1),
+            )
 
         def empty_pc(engine_copy, half, i):
             engine_copy(out=pc_sb[:, i, half * HALF : (half + 1) * HALF], in_=pc_bank[half, i][:])
@@ -143,13 +156,13 @@ def tile_mix_bilin_fm_pl_none_kernel(tc, x, wx, c, wc, w_words, w_scales, out_0,
                 op=mybir.AluOpType.mult,
             )
 
-        def project_h(e, bank):
-            y_bank[e, bank] = ps.tile([P, PACK, CHUNK], F32, name="y_%d_%d" % (e, bank), tag="bank%d" % bank)
-            for i in range(PACK):
+        def project_h(e, bank, first, count):
+            y_bank[e, first] = ps.tile([P, count, CHUNK], F32, name="y_%d_%d" % (e, first), tag="bank%d" % bank)
+            for i in range(first, first + count):
                 nc.tensor.matmul_mx(
-                    out=y_bank[e, bank][:, i, :],
+                    out=y_bank[e, first][:, i - first, :],
                     lhsT=w_words_dealt[:, 2 * i * P : 2 * (i + 1) * P].bitcast(E2M1),
-                    lhsT_scale=w_plane_dealt[:, i * P : (i + 1) * P],
+                    lhsT_scale=w_plane_dealt[:, i, :P],
                     rhs=h_words[e][:].bitcast(E4M3),
                     rhs_scale=h_plane[e][:],
                     start=True,
@@ -160,59 +173,30 @@ def tile_mix_bilin_fm_pl_none_kernel(tc, x, wx, c, wc, w_words, w_scales, out_0,
             h_words[e] = sb.tile([P, CHUNK], U32, name="h_words_%d" % e, align_bytes=64)
             h_plane[e] = sb.tile([P, CHUNK], U8, name="h_plane_%d" % e, align_bytes=64)
             nc.vector.quantize_mx(out=h_words[e][:].bitcast(E4M3), scales=h_plane[e][:], in_=h_rounded[e][:])
-            project_h(e, e)
 
-        def quantise_last_h(e, spare):
-            h_words[e] = sb.tile([P, CHUNK], U32, name="h_words_%d" % e, align_bytes=64)
-            h_plane[e] = sb.tile([P, CHUNK], U8, name="h_plane_%d" % e, align_bytes=64)
-            nc.vector.quantize_mx(out=h_words[e][:].bitcast(E4M3), scales=h_plane[e][:], in_=h_rounded[e][:])
-            for first, bank in ((0, e), (PAIR, spare)):
-                y_bank[e, bank] = ps.tile([P, PAIR, CHUNK], F32, name="y_%d_%d" % (e, bank), tag="bank%d" % bank)
-                for i in range(first, first + PAIR):
-                    nc.tensor.matmul_mx(
-                        out=y_bank[e, bank][:, i - first, :],
-                        lhsT=w_words_dealt[:, 2 * i * P : 2 * (i + 1) * P].bitcast(E2M1),
-                        lhsT_scale=w_plane_dealt[:, i * P : (i + 1) * P],
-                        rhs=h_words[e][:].bitcast(E4M3),
-                        rhs_scale=h_plane[e][:],
-                        start=True,
-                        stop=True,
-                    )
+        def copy_y(engine_copy, e, first=0, count=PACK):
+            engine_copy(out=y_sb[:, first : first + count, e * CHUNK : (e + 1) * CHUNK], in_=y_bank[e, first][:])
 
-        def copy_y_pair(engine_copy, e, bank, first):
-            engine_copy(out=y_sb[:, first : first + PAIR, e * CHUNK : (e + 1) * CHUNK], in_=y_bank[e, bank][:])
+        def y_rounded_at(t0, t1):
+            return y_rounded[:, PACK * t0 : PACK * t1]
 
-        def deal_w():
-            nc.vector.tensor_copy(
-                out=w_words_dealt[:].rearrange("p (i m b) -> p i m b", i=PACK, b=2),
-                in_=w_words_raw[:].rearrange("p (m i b) -> p i m b", i=PACK, b=2),
-            )
-            nc.vector.tensor_copy(
-                out=w_plane_dealt[:].rearrange("p (i m) -> p i m", i=PACK),
-                in_=w_plane_raw[:].rearrange("p (m i) -> p i m", i=PACK),
-            )
+        def round_y_from_psum(engine_copy, e):
+            dst = y_rounded_at(e * CHUNK, (e + 1) * CHUNK)
+            engine_copy(out=dst.rearrange("p (t i) -> p t i", i=PACK), in_=y_bank[e, 0][:].rearrange("p i t -> p t i"))
 
-        def copy_y(engine_copy, e, bank):
-            engine_copy(out=y_sb[:, :, e * CHUNK : (e + 1) * CHUNK], in_=y_bank[e, bank][:])
-
-        def round_y_from_psum(engine_copy, e, bank):
-            dst = y_rounded[:, PACK * e * CHUNK : PACK * (e + 1) * CHUNK]
-            engine_copy(out=dst.rearrange("p (t i) -> p t i", i=PACK), in_=y_bank[e, bank][:].rearrange("p i t -> p t i"))
-
-        def round_y_from_sbuf(engine_copy, first, last):
-            t0, t1 = first * CHUNK, (last + 1) * CHUNK
+        def round_y_from_sbuf(engine_copy, t0, t1):
             engine_copy(
-                out=y_rounded[:, PACK * t0 : PACK * t1].rearrange("p (c u i) -> p c i u", u=PAIR, i=PACK),
+                out=y_rounded_at(t0, t1).rearrange("p (c u i) -> p c i u", u=PAIR, i=PACK),
                 in_=y_sb[:, :, t0:t1].rearrange("p i (c u) -> p c i u", u=PAIR),
             )
 
         def quantise_y(first, last):
             t0, t1 = first * CHUNK, (last + 1) * CHUNK
-            k, column = divmod(t0, T // PACK)
+            k, column = divmod(t0, QUARTER)
             nc.vector.quantize_mx(
                 out=y_words[:, t0:t1].bitcast(E4M3),
                 scales=y_plane[4 * k :, column : column + t1 - t0],
-                in_=y_rounded[:, PACK * t0 : PACK * t1],
+                in_=y_rounded_at(t0, t1),
             )
 
         def store_values(queue, first, last):
@@ -231,34 +215,50 @@ def tile_mix_bilin_fm_pl_none_kernel(tc, x, wx, c, wc, w_words, w_scales, out_0,
 
         round_weight(on_vector, "wc", 0, 0)
         round_weight(on_scalar, "wc", 0, 2)
-        quantise("wc", 0, 0, R)
+        quantise("wc", 0, 0, 512)
         deal_w()
-        for g in range(PASSES):
-            for t0 in (0, HALF):
-                round_columns(on_vector, "c", g, t0, t0 + 320)
-                round_columns(on_scalar, "c", g, t0 + 320, t0 + HALF)
-            for half in range(2):
-                quantise("c", g, half * HALF, (half + 1) * HALF)
-                if g == 0:
-                    project_c(0, half)
+        round_columns(on_vector, "c", 0, 0, 320)
+        round_columns(on_scalar, "c", 0, 320, 512)
+        round_columns(on_vector, "c", 0, 512, 832)
+        round_columns(on_scalar, "c", 0, 832, 1024)
+        quantise("c", 0, 0, 512)
+        project_c(0, 0, 0)
+        project_c(0, 0, 1)
+        project_c(0, 0, 2)
+        project_c(0, 0, 3)
+        quantise("c", 0, 512, 1024)
+        project_c(0, 1, 0)
+        project_c(0, 1, 1)
+        project_c(0, 1, 2)
+        project_c(0, 1, 3)
+        round_columns(on_vector, "c", 1, 0, 320)
+        round_columns(on_scalar, "c", 1, 320, 512)
+        round_columns(on_vector, "c", 1, 512, 832)
+        round_columns(on_scalar, "c", 1, 832, 1024)
+        quantise("c", 1, 0, 512)
+        quantise("c", 1, 512, 1024)
         round_weight(on_vector, "wc", 1, 0)
         round_weight(on_scalar, "wc", 1, 2)
         quantise("wc", 1, 0, 256)
-        for half in range(2):
-            project_c(1, half, 0, PAIR)
+        project_c(1, 0, 0)
+        project_c(1, 0, 1)
+        project_c(1, 1, 0)
+        project_c(1, 1, 1)
         round_weight(on_vector, "wx", 0, 0)
         round_weight(on_scalar, "wx", 0, 2)
         empty_pc(on_vector, 0, 0)
         empty_pc(on_scalar, 0, 1)
-        quantise("wx", 0, 0, R)
+        quantise("wx", 0, 0, 512)
         round_weight(on_vector, "wx", 1, 0)
         round_weight(on_scalar, "wx", 1, 2)
-        quantise("wc", 1, 256, R)
-        for half in range(2):
-            project_c(1, half, PAIR, PAIR)
+        quantise("wc", 1, 256, 512)
+        project_c(1, 0, 2)
+        project_c(1, 0, 3)
+        project_c(1, 1, 2)
+        project_c(1, 1, 3)
         empty_pc(on_vector, 1, 1)
         empty_pc(on_scalar, 1, 0)
-        quantise("wx", 1, 0, R)
+        quantise("wx", 1, 0, 512)
         empty_pc(on_scalar, 0, 2)
         round_columns(on_vector, "x", 0, 0, 128)
         round_columns(on_vector, "x", 0, 128, 256)
@@ -288,54 +288,76 @@ def tile_mix_bilin_fm_pl_none_kernel(tc, x, wx, c, wc, w_words, w_scales, out_0,
         multiply(1)
         round_columns(on_scalar, "x", 0, 512, 768)
         quantise_h(0)
+        project_h(0, 0, 0, PACK)
         quantise("x", 1, 384, 512)
         project_x(1, 3)
         quantise_h(1)
-        for a in (2, 4):
-            b, na, nb = a + 1, a + 2, a + 3
-            multiply(a)
-            round_columns(on_scalar, "x", 1, na * CHUNK, nb * CHUNK)
-            quantise("x", 0, na * CHUNK, (nb + 1) * CHUNK)
-            project_x(0, na)
-            project_x(0, nb)
-            round_columns(on_vector, "x", 1, nb * CHUNK, (nb + 1) * CHUNK)
-            copy_y(on_scalar, a - 2, a - 2)
-            copy_y(on_scalar, b - 2, b - 2)
-            store_values(nc.sync, a - 2, b - 2)
-            quantise("x", 1, na * CHUNK, nb * CHUNK)
-            project_x(1, na)
-            quantise_h(a)
-            quantise("x", 1, nb * CHUNK, (nb + 1) * CHUNK)
-            project_x(1, nb)
-            multiply(b)
-            if a == 2:
-                round_columns(on_scalar, "x", 0, 768, 1024)
-            else:
-                round_y_from_psum(on_scalar, 1, 1)
-            round_y_from_sbuf(on_vector, (0, 3)[a // 4], (0, 3)[a // 4])
-            quantise_h(b)
+        project_h(1, 1, 0, PACK)
+        multiply(2)
+        round_columns(on_scalar, "x", 1, 512, 640)
+        quantise("x", 0, 512, 768)
+        project_x(0, 4)
+        project_x(0, 5)
+        round_columns(on_vector, "x", 1, 640, 768)
+        copy_y(on_scalar, 0)
+        copy_y(on_scalar, 1)
+        store_values(nc.sync, 0, 1)
+        quantise("x", 1, 512, 640)
+        project_x(1, 4)
+        quantise_h(2)
+        project_h(2, 2, 0, PACK)
+        quantise("x", 1, 640, 768)
+        project_x(1, 5)
+        multiply(3)
+        round_columns(on_scalar, "x", 0, 768, 1024)
+        round_y_from_sbuf(on_vector, 0, 128)
+        quantise_h(3)
+        project_h(3, 3, 0, PACK)
+        multiply(4)
+        round_columns(on_scalar, "x", 1, 768, 896)
+        quantise("x", 0, 768, 1024)
+        project_x(0, 6)
+        project_x(0, 7)
+        round_columns(on_vector, "x", 1, 896, 1024)
+        copy_y(on_scalar, 2)
+        copy_y(on_scalar, 3)
+        store_values(nc.sync, 2, 3)
+        quantise("x", 1, 768, 896)
+        project_x(1, 6)
+        quantise_h(4)
+        project_h(4, 4, 0, PACK)
+        quantise("x", 1, 896, 1024)
+        project_x(1, 7)
+        multiply(5)
+        round_y_from_psum(on_scalar, 1)
+        round_y_from_sbuf(on_vector, 384, 512)
+        quantise_h(5)
+        project_h(5, 5, 0, PACK)
         multiply(6)
-        round_y_from_psum(on_scalar, 2, 2)
-        copy_y(on_scalar, 4, 4)
+        round_y_from_psum(on_scalar, 2)
+        copy_y(on_scalar, 4)
         quantise_y(0, 1)
         store_words(nc.sync, 0, 1)
         quantise_h(6)
+        project_h(6, 6, 0, PACK)
         multiply(7)
-        copy_y(on_scalar, 5, 5)
+        copy_y(on_scalar, 5)
         store_values(nc.sync, 4, 5)
         quantise_y(2, 3)
         store_words(nc.sync, 2, 3)
-        quantise_last_h(7, 0)
-        round_y_from_psum(on_scalar, 4, 4)
-        round_y_from_sbuf(on_vector, 5, 5)
+        quantise_h(7)
+        project_h(7, 7, 0, PAIR)
+        project_h(7, 0, PAIR, PAIR)
+        round_y_from_psum(on_scalar, 4)
+        round_y_from_sbuf(on_vector, 640, 768)
         quantise_y(4, 5)
         store_words(nc.sync, 4, 5)
-        copy_y(on_scalar, 6, 6)
-        round_y_from_psum(on_scalar, 6, 6)
-        copy_y_pair(on_vector, 7, 7, 0)
-        copy_y_pair(on_scalar, 7, 0, 2)
+        copy_y(on_scalar, 6)
+        round_y_from_psum(on_scalar, 6)
+        copy_y(on_vector, 7, 0, PAIR)
+        copy_y(on_scalar, 7, 2, PAIR)
         store_values(nc.sync, 6, 7)
-        round_y_from_sbuf(on_vector, 7, 7)
+        round_y_from_sbuf(on_vector, 896, 1024)
         quantise_y(6, 7)
         store_scales(nc.scalar, 0)
         store_words(nc.sync, 6, 7)

@@ -350,13 +350,14 @@ def tile_mix_bilin_fm_pl_none_kernel(tc, x, wx, c, wc, w_words, w_scales, out_0,
         project_h(7, 0, PAIR, PAIR)
         round_y_from_psum(on_scalar, 4)
         round_y_from_sbuf(on_vector, 640, 768)
-        quantise_y(4, 5)
+        quantise_y(4, 4)
+        quantise_y(5, 5)
         store_words(nc.sync, 4, 5)
         copy_y(on_scalar, 6)
-        round_y_from_psum(on_scalar, 6)
         copy_y(on_vector, 7, 0, PAIR)
         copy_y(on_scalar, 7, 2, PAIR)
         store_values(nc.sync, 6, 7)
+        round_y_from_psum(on_scalar, 6)
         round_y_from_sbuf(on_vector, 896, 1024)
         quantise_y(6, 7)
         store_scales(nc.scalar, 0)

@@ -1,3 +1,4 @@
+import math
 from contextlib import ExitStack
 
 import concourse.mybir as mybir
@@ -25,6 +26,8 @@ RUN = 4
 PAIR = 2
 QUADS = 4
 
+ALIGN = 256
+SIZE = {F32: 4, U32: 4, BF16: 2, U8: 1}
 STEP = 32
 
 X_LOADS = [(0, 0, 512), (1, 0, 256), (1, 256, 256), (0, 512, 256), (1, 512, 256), (0, 768, 256), (1, 768, 256)]
@@ -37,26 +40,33 @@ def tile_mix_bilin_fm_pl_none_kernel(tc, x, wx, c, wc, w_words, w_scales, out_0,
         ps = ctx.enter_context(tc.psum_pool(name="ps", bufs=1))
         ctx.enter_context(tc.manual_schedule())
 
+        taken = [0]
+
+        def sbuf_tile(shape, dtype, name):
+            offset = taken[0]
+            taken[0] = offset + -(-math.prod(shape[1:]) * SIZE[dtype] // ALIGN) * ALIGN
+            return sb.tile(shape, dtype, name=name, align_bytes=ALIGN, offset=offset)
+
         landed_in, rounded, words, planes = {}, {}, {}, {}
         for name, width in (("wc", R), ("c", T), ("wx", R), ("x", T)):
             for g in range(PASSES):
-                rounded[name, g] = sb.tile([P, PACK * width], BF16, name="rounded_%s_%d" % (name, g), align_bytes=64)
-                words[name, g] = sb.tile([P, width], U32, name="words_%s_%d" % (name, g), align_bytes=64)
-                planes[name, g] = sb.tile([P, width], U8, name="plane_%s_%d" % (name, g), align_bytes=64)
+                rounded[name, g] = sbuf_tile([P, PACK * width], BF16, "rounded_%s_%d" % (name, g))
+                words[name, g] = sbuf_tile([P, width], U32, "words_%s_%d" % (name, g))
+                planes[name, g] = sbuf_tile([P, width], U8, "plane_%s_%d" % (name, g))
 
         def load(name, src, g, t0, width):
-            landed = sb.tile([P, PACK, width], F32, name="raw_%s_%d_%d" % (name, g, t0))
+            landed = sbuf_tile([P, PACK, width], F32, "raw_%s_%d_%d" % (name, g, t0))
             rows = src[g * K_PASS : (g + 1) * K_PASS, t0 : t0 + width]
             nc.sync.dma_start(out=landed[:], in_=rows.rearrange("(p j) w -> p j w", j=PACK))
             for t in range(t0, t0 + width, STEP):
                 landed_in[name, g, t // STEP] = (landed, t0)
 
-        w_plane_raw = sb.tile([P, M], U8, name="w_plane_raw", align_bytes=64)
+        w_plane_raw = sbuf_tile([P, M], U8, "w_plane_raw")
         nc.vector.memset(w_plane_raw[:].bitcast(I32), 0)
 
         load("wc", wc, 0, 0, R)
 
-        w_words_raw = sb.tile([P, 2 * M], U8, name="w_words_raw", align_bytes=64)
+        w_words_raw = sbuf_tile([P, 2 * M], U8, "w_words_raw")
         nc.sync.dma_start(out=w_words_raw[:].bitcast(I32), in_=w_words[0].bitcast(I32))
         for quad in range(QUADS):
             nc.sync.dma_start(
@@ -94,14 +104,14 @@ def tile_mix_bilin_fm_pl_none_kernel(tc, x, wx, c, wc, w_words, w_scales, out_0,
             )
 
         pc_bank, px_bank, y_bank = {}, {}, {}
-        pc_sb = sb.tile([P, PACK, T], F32, name="pc_sb")
-        y_sb = sb.tile([P, PACK, T], F32, name="y_sb")
-        y_rounded = sb.tile([P, PACK * T], BF16, name="y_rounded", align_bytes=64)
-        y_words = sb.tile([P, T], U32, name="y_words", align_bytes=64)
-        y_plane = sb.tile([P, T // PACK], U8, name="y_plane", align_bytes=64)
+        pc_sb = sbuf_tile([P, PACK, T], F32, "pc_sb")
+        y_sb = sbuf_tile([P, PACK, T], F32, "y_sb")
+        y_rounded = sbuf_tile([P, PACK * T], BF16, "y_rounded")
+        y_words = sbuf_tile([P, T], U32, "y_words")
+        y_plane = sbuf_tile([P, T // PACK], U8, "y_plane")
         h_rounded, h_words, h_plane = {}, {}, {}
-        w_words_dealt = sb.tile([P, 2 * M], U8, name="w_words_dealt", align_bytes=64)
-        w_plane_dealt = sb.tile([P, PACK, 2 * P], U8, name="w_plane_dealt", align_bytes=64)
+        w_words_dealt = sbuf_tile([P, 2 * M], U8, "w_words_dealt")
+        w_plane_dealt = sbuf_tile([P, PACK, 2 * P], U8, "w_plane_dealt")
 
         def deal_w():
             nc.vector.tensor_copy(
@@ -148,7 +158,7 @@ def tile_mix_bilin_fm_pl_none_kernel(tc, x, wx, c, wc, w_words, w_scales, out_0,
                 )
 
         def multiply(e):
-            h_rounded[e] = sb.tile([P, PACK * CHUNK], BF16, name="h_rounded_%d" % e, align_bytes=64)
+            h_rounded[e] = sbuf_tile([P, PACK * CHUNK], BF16, "h_rounded_%d" % e)
             nc.vector.tensor_tensor(
                 out=h_rounded[e][:].rearrange("p (c u i) -> p c i u", u=RUN, i=PACK),
                 in0=px_bank[e][:].rearrange("p i (c u) -> p c i u", u=RUN),
@@ -170,8 +180,8 @@ def tile_mix_bilin_fm_pl_none_kernel(tc, x, wx, c, wc, w_words, w_scales, out_0,
                 )
 
         def quantise_h(e):
-            h_words[e] = sb.tile([P, CHUNK], U32, name="h_words_%d" % e, align_bytes=64)
-            h_plane[e] = sb.tile([P, CHUNK], U8, name="h_plane_%d" % e, align_bytes=64)
+            h_words[e] = sbuf_tile([P, CHUNK], U32, "h_words_%d" % e)
+            h_plane[e] = sbuf_tile([P, CHUNK], U8, "h_plane_%d" % e)
             nc.vector.quantize_mx(out=h_words[e][:].bitcast(E4M3), scales=h_plane[e][:], in_=h_rounded[e][:])
 
         def copy_y(engine_copy, e, first=0, count=PACK):

@@ -27,6 +27,8 @@ PAIR = 2
 QUADS = 4
 
 ALIGN = 256
+DMA_ALIGN = 2048
+DMA_BYTES = 116 * 1024
 SIZE = {F32: 4, U32: 4, BF16: 2, U8: 1}
 STEP = 32
 
@@ -40,12 +42,12 @@ def tile_mix_bilin_fm_pl_none_kernel(tc, x, wx, c, wc, w_words, w_scales, out_0,
         ps = ctx.enter_context(tc.psum_pool(name="ps", bufs=1))
         ctx.enter_context(tc.manual_schedule())
 
-        taken = [0]
+        taken = {ALIGN: DMA_BYTES, DMA_ALIGN: 0}
 
-        def sbuf_tile(shape, dtype, name):
-            offset = taken[0]
-            taken[0] = offset + -(-math.prod(shape[1:]) * SIZE[dtype] // ALIGN) * ALIGN
-            return sb.tile(shape, dtype, name=name, align_bytes=ALIGN, offset=offset)
+        def sbuf_tile(shape, dtype, name, align=ALIGN):
+            offset = taken[align]
+            taken[align] = offset + -(-math.prod(shape[1:]) * SIZE[dtype] // align) * align
+            return sb.tile(shape, dtype, name=name, align_bytes=align, offset=offset)
 
         landed_in, rounded, words, planes = {}, {}, {}, {}
         for name, width in (("wc", R), ("c", T), ("wx", R), ("x", T)):
@@ -55,7 +57,7 @@ def tile_mix_bilin_fm_pl_none_kernel(tc, x, wx, c, wc, w_words, w_scales, out_0,
                 planes[name, g] = sbuf_tile([P, width], U8, "plane_%s_%d" % (name, g))
 
         def load(name, src, g, t0, width):
-            landed = sbuf_tile([P, PACK, width], F32, "raw_%s_%d_%d" % (name, g, t0))
+            landed = sbuf_tile([P, PACK, width], F32, "raw_%s_%d_%d" % (name, g, t0), DMA_ALIGN)
             rows = src[g * K_PASS : (g + 1) * K_PASS, t0 : t0 + width]
             nc.sync.dma_start(out=landed[:], in_=rows.rearrange("(p j) w -> p j w", j=PACK))
             for t in range(t0, t0 + width, STEP):
@@ -105,9 +107,9 @@ def tile_mix_bilin_fm_pl_none_kernel(tc, x, wx, c, wc, w_words, w_scales, out_0,
 
         pc_bank, px_bank, y_bank = {}, {}, {}
         pc_sb = sbuf_tile([P, PACK, T], F32, "pc_sb")
-        y_sb = sbuf_tile([P, PACK, T], F32, "y_sb")
+        y_sb = sbuf_tile([P, PACK, T], F32, "y_sb", DMA_ALIGN)
         y_rounded = sbuf_tile([P, PACK * T], BF16, "y_rounded")
-        y_words = sbuf_tile([P, T], U32, "y_words")
+        y_words = sbuf_tile([P, T], U32, "y_words", DMA_ALIGN)
         y_plane = sbuf_tile([P, T // PACK], U8, "y_plane")
         h_rounded, h_words, h_plane = {}, {}, {}
         w_words_dealt = sbuf_tile([P, 2 * M], U8, "w_words_dealt")

@@ -93,8 +93,9 @@ def tile_mix_bilin_fm_pl_none_kernel(tc, x, wx, c, wc, w_words, w_scales, out_0,
 
         def round_columns(engine_copy, name, g, t0, t1):
             landed, first = landed_in[name, g, t0 // STEP]
-            dst = rounded[name, g][:, PACK * t0 : PACK * t1].rearrange("p (c i j) -> p c j i", i=PAIR, j=PACK)
-            src = landed[:, :, t0 - first : t1 - first].rearrange("p j (c i) -> p c j i", i=PAIR)
+            run = PACK if engine_copy is on_scalar else PAIR
+            dst = rounded[name, g][:, PACK * t0 : PACK * t1].rearrange("p (c i j) -> p c j i", i=run, j=PACK)
+            src = landed[:, :, t0 - first : t1 - first].rearrange("p j (c i) -> p c j i", i=run)
             engine_copy(out=dst, in_=src)
 
         def quantise(name, g, t0, t1):

import math
from contextlib import ExitStack

import concourse.mybir as mybir

K, L, R, M, T = 1024, 1024, 512, 512, 1024
FLOPS = 2 * T * (K * R + L * R + R * M)

F32 = mybir.dt.float32
BF16 = mybir.dt.bfloat16
I32 = mybir.dt.int32
U32 = mybir.dt.uint32
U8 = mybir.dt.uint8
E4M3 = mybir.dt.float8_e4m3fn_x4
E5M2 = mybir.dt.float8_e5m2_x4
E2M1 = mybir.dt.float4_e2m1fn_x4

P = 128
PACK = 4
K_PASS = P * PACK
PASSES = K // K_PASS
HALF = 512
QUARTER = 256
CHUNK = 128
RUN = 4
PAIR = 2
QUADS = 4

ALIGN = 256
DMA_ALIGN = 2048
DMA_BYTES = 116 * 1024
SIZE = {F32: 4, U32: 4, BF16: 2, U8: 1}
STEP = 32

X_LOADS = [(0, 0, 512), (1, 0, 256), (1, 256, 256), (0, 512, 256), (1, 512, 256), (0, 768, 256), (1, 768, 256)]


def tile_mix_bilin_fm_pl_none_kernel(tc, x, wx, c, wc, w_words, w_scales, out_0, out_1, out_2):
    nc = tc.nc
    with ExitStack() as ctx:
        sb = ctx.enter_context(tc.tile_pool(name="sb", bufs=1))
        ps = ctx.enter_context(tc.psum_pool(name="ps", bufs=1))
        ctx.enter_context(tc.manual_schedule())

        taken = {ALIGN: DMA_BYTES, DMA_ALIGN: 0}

        def sbuf_tile(shape, dtype, name, align=ALIGN):
            offset = taken[align]
            taken[align] = offset + -(-math.prod(shape[1:]) * SIZE[dtype] // align) * align
            return sb.tile(shape, dtype, name=name, align_bytes=align, offset=offset)

        landed_in, rounded, words, planes = {}, {}, {}, {}
        for name, width in (("wc", R), ("c", T), ("wx", R), ("x", T)):
            for g in range(PASSES):
                rounded[name, g] = sbuf_tile([P, PACK * width], BF16, "rounded_%s_%d" % (name, g))
                words[name, g] = sbuf_tile([P, width], U32, "words_%s_%d" % (name, g))
                planes[name, g] = sbuf_tile([P, width], U8, "plane_%s_%d" % (name, g))

        def load(name, src, g, t0, width):
            landed = sbuf_tile([P, PACK, width], F32, "raw_%s_%d_%d" % (name, g, t0), DMA_ALIGN)
            rows = src[g * K_PASS : (g + 1) * K_PASS, t0 : t0 + width]
            nc.sync.dma_start(out=landed[:], in_=rows.rearrange("(p j) w -> p j w", j=PACK))
            for t in range(t0, t0 + width, STEP):
                landed_in[name, g, t // STEP] = (landed, t0)

        w_plane_raw = sbuf_tile([P, M], U8, "w_plane_raw")
        nc.vector.memset(w_plane_raw[:].bitcast(I32), 0)

        load("wc", wc, 0, 0, R)

        w_words_raw = sbuf_tile([P, 2 * M], U8, "w_words_raw")
        nc.sync.dma_start(out=w_words_raw[:].bitcast(I32), in_=w_words[0].bitcast(I32))
        for quad in range(QUADS):
            nc.sync.dma_start(
                out=w_plane_raw[32 * quad : 32 * quad + 4, :].bitcast(I32),
                in_=w_scales[0, 4 * quad : 4 * quad + 4, :].bitcast(I32),
            )

        for g in range(PASSES):
            load("c", c, g, 0, T)
        load("wc", wc, 1, 0, R)
        for g in range(PASSES):
            load("wx", wx, g, 0, R)
        for g, t0, width in X_LOADS:
            load("x", x, g, t0, width)

        on_vector, on_scalar = nc.vector.tensor_copy, nc.scalar.copy

        def round_weight(engine_copy, name, g, first):
            dst = rounded[name, g][:].rearrange("p (i m j) -> p m j i", i=PACK, j=PACK)
            src = landed_in[name, g, 0][0][:].rearrange("p j (m i) -> p m j i", i=PACK)
            engine_copy(out=dst[:, :, :, first : first + PAIR], in_=src[:, :, :, first : first + PAIR])

        def round_columns(engine_copy, name, g, t0, t1):
            landed, first = landed_in[name, g, t0 // STEP]
            run = PACK if engine_copy is on_scalar else PAIR
            dst = rounded[name, g][:, PACK * t0 : PACK * t1].rearrange("p (c i j) -> p c j i", i=run, j=PACK)
            src = landed[:, :, t0 - first : t1 - first].rearrange("p j (c i) -> p c j i", i=run)
            engine_copy(out=dst, in_=src)

        def quantise(name, g, t0, t1):
            fmt = E5M2 if name == "c" else E4M3
            nc.vector.quantize_mx(
                out=words[name, g][:, t0:t1].bitcast(fmt),
                scales=planes[name, g][:, t0:t1],
                in_=rounded[name, g][:, PACK * t0 : PACK * t1],
            )

        pc_bank, px_bank, y_bank = {}, {}, {}
        pc_sb = sbuf_tile([P, PACK, T], F32, "pc_sb")
        y_sb = sbuf_tile([P, PACK, T], F32, "y_sb", DMA_ALIGN)
        y_rounded = sbuf_tile([P, PACK * T], BF16, "y_rounded")
        y_words = sbuf_tile([P, T], U32, "y_words", DMA_ALIGN)
        y_plane = sbuf_tile([P, T // PACK], U8, "y_plane")
        h_rounded, h_words, h_plane = {}, {}, {}
        w_words_dealt = sbuf_tile([P, 2 * M], U8, "w_words_dealt")
        w_plane_dealt = sbuf_tile([P, PACK, 2 * P], U8, "w_plane_dealt")

        def deal_w():
            nc.vector.tensor_copy(
                out=w_words_dealt[:].rearrange("p (i m b) -> p i m b", i=PACK, b=2),
                in_=w_words_raw[:].rearrange("p (m i b) -> p i m b", i=PACK, b=2),
            )
            nc.vector.tensor_copy(
                out=w_plane_dealt[:, :, :P],
                in_=w_plane_raw[:].rearrange("p (m i) -> p i m", i=PACK),
            )

        def project_c(g, half, i):
            if g == 0:
                pc_bank[half, i] = ps.tile([P, HALF], F32, name="pc_%d_%d" % (half, i), tag="bank%d" % (PACK * half + i))
            dealt = slice(i * P, (i + 1) * P)
            cols = slice(half * HALF, (half + 1) * HALF)
            nc.tensor.matmul_mx(
                out=pc_bank[half, i][:],
                lhsT=words["wc", g][:, dealt].bitcast(E4M3),
                lhsT_scale=planes["wc", g][:, dealt],
                rhs=words["c", g][:, cols].bitcast(E5M2),
                rhs_scale=planes["c", g][:, cols],
                start=(g == 0),
                stop=(g == PASSES - 1),
            )

        def empty_pc(engine_copy, half, i):
            engine_copy(out=pc_sb[:, i, half * HALF : (half + 1) * HALF], in_=pc_bank[half, i][:])

        def project_x(g, e):
            if g == 0:
                px_bank[e] = ps.tile([P, PACK, CHUNK], F32, name="px_%d" % e, tag="bank%d" % e)
            cols = slice(e * CHUNK, (e + 1) * CHUNK)
            for i in range(PACK):
                dealt = slice(i * P, (i + 1) * P)
                nc.tensor.matmul_mx(
                    out=px_bank[e][:, i, :],
                    lhsT=words["wx", g][:, dealt].bitcast(E4M3),
                    lhsT_scale=planes["wx", g][:, dealt],
                    rhs=words["x", g][:, cols].bitcast(E4M3),
                    rhs_scale=planes["x", g][:, cols],
                    start=(g == 0 and i == 0),
                    stop=(g == PASSES - 1 and i == PACK - 1),
                )

        def multiply(e):
            h_rounded[e] = sbuf_tile([P, PACK * CHUNK], BF16, "h_rounded_%d" % e)
            nc.vector.tensor_tensor(
                out=h_rounded[e][:].rearrange("p (c u i) -> p c i u", u=RUN, i=PACK),
                in0=px_bank[e][:].rearrange("p i (c u) -> p c i u", u=RUN),
                in1=pc_sb[:, :, e * CHUNK : (e + 1) * CHUNK].rearrange("p i (c u) -> p c i u", u=RUN),
                op=mybir.AluOpType.mult,
            )

        def project_h(e, bank, first, count):
            y_bank[e, first] = ps.tile([P, count, CHUNK], F32, name="y_%d_%d" % (e, first), tag="bank%d" % bank)
            for i in range(first, first + count):
                nc.tensor.matmul_mx(
                    out=y_bank[e, first][:, i - first, :],
                    lhsT=w_words_dealt[:, 2 * i * P : 2 * (i + 1) * P].bitcast(E2M1),
                    lhsT_scale=w_plane_dealt[:, i, :P],
                    rhs=h_words[e][:].bitcast(E4M3),
                    rhs_scale=h_plane[e][:],
                    start=True,
                    stop=True,
                )

        def quantise_h(e):
            h_words[e] = sbuf_tile([P, CHUNK], U32, "h_words_%d" % e)
            h_plane[e] = sbuf_tile([P, CHUNK], U8, "h_plane_%d" % e)
            nc.vector.quantize_mx(out=h_words[e][:].bitcast(E4M3), scales=h_plane[e][:], in_=h_rounded[e][:])

        def copy_y(engine_copy, e, first=0, count=PACK):
            engine_copy(out=y_sb[:, first : first + count, e * CHUNK : (e + 1) * CHUNK], in_=y_bank[e, first][:])

        def y_rounded_at(t0, t1):
            return y_rounded[:, PACK * t0 : PACK * t1]

        def round_y_from_psum(engine_copy, e):
            dst = y_rounded_at(e * CHUNK, (e + 1) * CHUNK)
            engine_copy(out=dst.rearrange("p (t i) -> p t i", i=PACK), in_=y_bank[e, 0][:].rearrange("p i t -> p t i"))

        def round_y_from_sbuf(engine_copy, t0, t1):
            engine_copy(
                out=y_rounded_at(t0, t1).rearrange("p (c u i) -> p c i u", u=PAIR, i=PACK),
                in_=y_sb[:, :, t0:t1].rearrange("p i (c u) -> p c i u", u=PAIR),
            )

        def quantise_y(first, last):
            t0, t1 = first * CHUNK, (last + 1) * CHUNK
            k, column = divmod(t0, QUARTER)
            nc.vector.quantize_mx(
                out=y_words[:, t0:t1].bitcast(E4M3),
                scales=y_plane[4 * k :, column : column + t1 - t0],
                in_=y_rounded_at(t0, t1),
            )

        def store_values(queue, first, last):
            cols = slice(first * CHUNK, (last + 1) * CHUNK)
            queue.dma_start(out=out_0.rearrange("(p i) t -> p i t", i=PACK)[:, :, cols], in_=y_sb[:, :, cols])

        def store_words(queue, first, last):
            cols = slice(first * CHUNK, (last + 1) * CHUNK)
            queue.dma_start(out=out_1[0].rearrange("p t i -> p (t i)").bitcast(I32)[:, cols], in_=y_words[:, cols].bitcast(I32))

        def store_scales(queue, quad):
            queue.dma_start(
                out=out_2[0, 4 * quad : 4 * quad + 4, :].bitcast(I32).rearrange("s (k c) -> k s c", k=PACK),
                in_=y_plane[32 * quad : 32 * quad + 16, :].bitcast(I32),
            )

        round_weight(on_vector, "wc", 0, 0)
        round_weight(on_scalar, "wc", 0, 2)
        quantise("wc", 0, 0, 512)
        deal_w()
        round_columns(on_vector, "c", 0, 0, 320)
        round_columns(on_scalar, "c", 0, 320, 512)
        round_columns(on_vector, "c", 0, 512, 832)
        round_columns(on_scalar, "c", 0, 832, 1024)
        quantise("c", 0, 0, 512)
        project_c(0, 0, 0)
        project_c(0, 0, 1)
        project_c(0, 0, 2)
        project_c(0, 0, 3)
        quantise("c", 0, 512, 1024)
        project_c(0, 1, 0)
        project_c(0, 1, 1)
        project_c(0, 1, 2)
        project_c(0, 1, 3)
        round_columns(on_vector, "c", 1, 0, 320)
        round_columns(on_scalar, "c", 1, 320, 512)
        round_columns(on_vector, "c", 1, 512, 832)
        round_columns(on_scalar, "c", 1, 832, 1024)
        quantise("c", 1, 0, 512)
        quantise("c", 1, 512, 1024)
        round_weight(on_vector, "wc", 1, 0)
        round_weight(on_scalar, "wc", 1, 2)
        quantise("wc", 1, 0, 256)
        project_c(1, 0, 0)
        project_c(1, 0, 1)
        project_c(1, 1, 0)
        project_c(1, 1, 1)
        round_weight(on_vector, "wx", 0, 0)
        round_weight(on_scalar, "wx", 0, 2)
        empty_pc(on_vector, 0, 0)
        empty_pc(on_scalar, 0, 1)
        quantise("wx", 0, 0, 512)
        round_weight(on_vector, "wx", 1, 0)
        round_weight(on_scalar, "wx", 1, 2)
        quantise("wc", 1, 256, 512)
        project_c(1, 0, 2)
        project_c(1, 0, 3)
        project_c(1, 1, 2)
        project_c(1, 1, 3)
        empty_pc(on_vector, 1, 1)
        empty_pc(on_scalar, 1, 0)
        quantise("wx", 1, 0, 512)
        empty_pc(on_scalar, 0, 2)
        round_columns(on_vector, "x", 0, 0, 128)
        round_columns(on_vector, "x", 0, 128, 256)
        round_columns(on_scalar, "x", 0, 256, 384)
        quantise("x", 0, 0, 128)
        project_x(0, 0)
        round_columns(on_vector, "x", 0, 384, 512)
        quantise("x", 0, 128, 256)
        project_x(0, 1)
        empty_pc(on_scalar, 0, 3)
        empty_pc(on_scalar, 1, 2)
        round_columns(on_vector, "x", 1, 0, 128)
        round_columns(on_vector, "x", 1, 128, 256)
        quantise("x", 1, 0, 128)
        project_x(1, 0)
        quantise("x", 0, 256, 512)
        project_x(0, 2)
        quantise("x", 1, 128, 256)
        project_x(1, 1)
        project_x(0, 3)
        round_columns(on_scalar, "x", 1, 256, 384)
        round_columns(on_vector, "x", 1, 384, 512)
        empty_pc(on_scalar, 1, 3)
        multiply(0)
        quantise("x", 1, 256, 384)
        project_x(1, 2)
        multiply(1)
        round_columns(on_scalar, "x", 0, 512, 768)
        quantise_h(0)
        project_h(0, 0, 0, PACK)
        quantise("x", 1, 384, 512)
        project_x(1, 3)
        quantise_h(1)
        project_h(1, 1, 0, PACK)
        multiply(2)
        round_columns(on_scalar, "x", 1, 512, 640)
        quantise("x", 0, 512, 768)
        project_x(0, 4)
        project_x(0, 5)
        round_columns(on_vector, "x", 1, 640, 768)
        copy_y(on_scalar, 0)
        copy_y(on_scalar, 1)
        store_values(nc.sync, 0, 1)
        quantise("x", 1, 512, 640)
        project_x(1, 4)
        quantise_h(2)
        project_h(2, 2, 0, PACK)
        quantise("x", 1, 640, 768)
        project_x(1, 5)
        multiply(3)
        round_columns(on_scalar, "x", 0, 768, 1024)
        round_y_from_sbuf(on_vector, 0, 128)
        quantise_h(3)
        project_h(3, 3, 0, PACK)
        multiply(4)
        round_columns(on_scalar, "x", 1, 768, 896)
        quantise("x", 0, 768, 1024)
        project_x(0, 6)
        project_x(0, 7)
        round_columns(on_vector, "x", 1, 896, 1024)
        copy_y(on_scalar, 2)
        copy_y(on_scalar, 3)
        store_values(nc.sync, 2, 3)
        quantise("x", 1, 768, 896)
        project_x(1, 6)
        quantise_h(4)
        project_h(4, 4, 0, PACK)
        quantise("x", 1, 896, 1024)
        project_x(1, 7)
        multiply(5)
        round_y_from_psum(on_scalar, 1)
        round_y_from_sbuf(on_vector, 384, 512)
        quantise_h(5)
        project_h(5, 5, 0, PACK)
        multiply(6)
        round_y_from_psum(on_scalar, 2)
        copy_y(on_scalar, 4)
        quantise_y(0, 1)
        store_words(nc.sync, 0, 1)
        quantise_h(6)
        project_h(6, 6, 0, PACK)
        multiply(7)
        copy_y(on_scalar, 5)
        store_values(nc.sync, 4, 5)
        quantise_y(2, 3)
        store_words(nc.sync, 2, 3)
        quantise_h(7)
        project_h(7, 7, 0, PAIR)
        project_h(7, 0, PAIR, PAIR)
        round_y_from_psum(on_scalar, 4)
        round_y_from_sbuf(on_vector, 640, 768)
        quantise_y(4, 4)
        quantise_y(5, 5)
        store_words(nc.sync, 4, 5)
        copy_y(on_scalar, 6)
        copy_y(on_vector, 7, 0, PAIR)
        copy_y(on_scalar, 7, 2, PAIR)
        store_values(nc.sync, 6, 7)
        round_y_from_psum(on_scalar, 6)
        round_y_from_sbuf(on_vector, 896, 1024)
        quantise_y(6, 7)
        store_scales(nc.scalar, 0)
        store_words(nc.sync, 6, 7)
        store_scales(nc.scalar, 1)
        store_scales(nc.sync, 2)
        store_scales(nc.sync, 3)
